import numpy as np, ml_dtypes
CORES = [66,74,82,90,194,202,210,218]
N = 8
BF = ml_dtypes.bfloat16
LA, SUB, W, V, VIS, TRY, R1, R2 = 128, 8, 1024, 4096, 5, 2, 9, 12
A = [5, 4, 4, 3, 3]
def levels(rng, n, lo, hi):
    return np.minimum((np.exp2(lo + (hi - lo) * rng.random((N, 8, 1, n))) * rng.random((N, 8, 16, n))).astype(np.int64), 255)
def slots(rng):
    share = rng.choice(np.array([0.3, 0.6, 0.9, 1.0]), (N, 8, 1, LA))
    return np.where(rng.random((N, 8, 16, LA)) < share, rng.integers(0, W, (N, 8, 16, LA)), -1)
def parts(rng):
    return (levels(rng, W, 6.5, 9.0), levels(rng, V, 5.5, 9.0), slots(rng), levels(rng, LA, 6.5, 9.0), rng.integers(1, 256, (N, 8, 16)), rng.integers(0, 256, (N, 8, 16)))
def pack(x, c, s, z, w, p):
    b = lambda v: np.ascontiguousarray(v.reshape(N, 128, -1)).astype(np.float32).astype(BF)
    i = lambda v: np.ascontiguousarray(v.reshape(N, 128, -1)).astype(np.int32)
    return {"x0": b(x), "cl": b(c), "sl": i(s), "z0": b(z), "wt": i(w), "kp": i(p)}
def setup_inputs(rng):
    return pack(*parts(rng))
def setup_inputs_spread(rng):
    x, c, s, z, w, p = parts(rng)
    x, c, z = levels(rng, W, 0.0, 9.0), levels(rng, V, 0.0, 9.0), levels(rng, LA, 0.0, 9.0)
    w = np.clip(np.exp2(8 * rng.random(w.shape)).astype(np.int64), 1, 255); p = np.clip(np.exp2(8 * rng.random(p.shape)).astype(np.int64) - 1, 0, 255)
    return pack(x, c, s, z, w, p)
def setup_inputs_ends(rng):
    e = lambda n, d: 255 * (rng.random((N, 8, 16, n)) < rng.choice(np.array(d), (N, 8, 1, n))).astype(np.int64)
    x, c, z = e(W, [0.3, 0.6, 0.9]), e(V, [0.0, 0.5, 0.9, 1.0]), e(LA, [0.3, 0.6, 0.9])
    r = rng.random((N, 8, 16, LA))
    s = np.where(r < 0.35, -1, np.where(r < 0.7, W - 1, np.where(r < 0.8, 0, rng.integers(0, W, r.shape))))
    w = np.where(rng.random((N, 8, 16)) < 0.5, 1, 255); w[:, :, 13:15] = 1; w[:, :, 15] = 255; w[:, 6] = 255
    p = 255 * rng.integers(0, 2, (N, 8, 16)); p[:, 7, 0] = 255; p[:, 7, 15] = 255; p[:, 7, 1] = 0
    x[..., W - 1] = 255
    for i in (0, LA - 1):
        z[..., i] = 0; z[:, :, 13:, i] = 255; s[:, :, 0, i] = W - 1
    for i in (1, LA - 2): z[..., i] = 255
    for i in (2, LA - 3): z[..., i] = 0
    return pack(x, c, s, z, w, p)
def setup_inputs_corners(rng):
    x, c, s, z, w, p = parts(rng); x[..., 0] = 255; x[..., W - 1] = 0
    kind = rng.integers(0, 10, (N, 8, 1, LA)); kind[..., :10] = np.arange(10); kind[..., LA - 10:] = np.arange(10)
    k = np.arange(16)[:, None]; o = np.argsort(rng.random((N, 8, 16, LA)), axis=2); any_ = rng.integers(0, W, s.shape)
    low = np.arange(LA) < LA // 2
    s = np.where(kind == 0, -1, s); s = np.where(kind == 1, any_, s)
    s = np.where(kind == 2, np.where(k == np.where(low, 13, 15), 0, W - 1), s)
    s = np.where(kind == 3, np.where(o < TRY, 0, W - 1), s); s = np.where(kind == 4, np.where(o < TRY + 1, 0, W - 1), s)
    s = np.where(kind == 5, np.where(k == 15, any_, -1), s); s = np.where(kind == 6, np.where(k == 15, -1, any_), s)
    s = np.where(kind == 7, SUB * np.arange(LA) + any_ % SUB, s); s = np.where(kind == 8, any_[:, :, :1], s)
    z = np.where(kind == 1, 255, z); z = np.where((kind >= 2) & (kind <= 4), np.minimum(z, 254), z); z = np.where((kind == 2) & low, 254, z)
    for q in range(N):
        g = rng.permutation(8)
        c[q, g[:2]] = 0; c[q, g[2:4]] = 255
        w[q, g[0]] = 1; w[q, g[2]] = 255; w[q, g[4]] = 255; w[q, g[5]] = 1; p[q, g[3]] = 0; p[q, g[5]] = 255; p[q, g[6]] = 0
    return pack(x, c, s, z, w, p)
def setup_inputs_ties(rng):
    x, c, s, z, w, p = parts(rng)
    x, c, z = 85 * (x >> 6), 85 * (c >> 6), 85 * (z >> 6)
    x[..., 1::2] = x[..., ::2]
    same = np.take_along_axis(x, np.maximum(s[:, :, 3:4], 0), 3)
    z = np.where(rng.random((N, 8, 1, LA)) < 0.5, same, z)
    return pack(x, c, s, z, w, p)
def setup_inputs_bits(rng):
    x, c, s, z, w, p = parts(rng); k = np.arange(16)[:, None]
    one = k == rng.integers(0, 16, (N, 8, 1, 1))
    x[..., 0] = 255; x[..., W - 2] = 0; x[..., W - 1:] = np.where(one, 255, 0)
    kind = rng.choice(np.array([0, 0, 1, 2, 3, 3]), (N, 1, 1, LA))
    m = np.where(kind == 0, 8, 1 + 2 * rng.integers(0, 4, kind.shape)); on = np.argsort(rng.random((N, 8, 1, LA)), axis=1) < m
    first = np.where(kind == 1, 0, TRY - 1)
    v = np.where(k < first, W - 1, np.where(k == first, 0, s))
    v = np.where(on, v, np.where(rng.random((N, 8, 1, LA)) < 0.5, -1, W - 2))
    s = np.where(kind < 3, v, s)
    high = 255 - (rng.random((N, 8, 16, LA)) < rng.choice(np.array([0.0, 0.5, 1.0]), (N, 1, 1, LA))).astype(np.int64)
    z = np.where(kind < 3, np.where(one, 254, high), z)
    w[:, 7] = 255
    return pack(x, c, s, z, w, p)
def check_inputs(d):
    bad = []
    for k, lo, hi in (("x0", 0, 255), ("cl", 0, 255), ("sl", -1, W - 1), ("z0", 0, 255), ("wt", 1, 255), ("kp", 0, 255)):
        v = np.asarray(d[k]).astype(np.float32)
        if np.min(v) < lo or np.max(v) > hi or np.any(v != np.floor(v)): bad.append("range of " + k)
    return bad
def hashes(v, w, p, t):
    u = np.add.reduce(w * v, axis=2) & (V - 1)
    return u, ((u * u >> 5)[:, :, None] + p * u[:, :, None] + 97 * t) & (V - 1)
def reference(x0, cl, sl, z0, wt, kp):
    x = x0.astype(np.float32).astype(np.int32).reshape(N, 8, 16, W); c = cl.astype(np.float32).astype(np.int32).reshape(N, 8, 16, V)
    z = z0.astype(np.float32).astype(np.int32).reshape(N, 8, 16, LA); s = sl.astype(np.int32).reshape(N, 8, 16, LA)
    w = wt.astype(np.int32).reshape(N, 8, 16, 1); p = kp.astype(np.int32).reshape(N, 8, 16, 1)
    bit = np.zeros((N, LA), np.int64); k16 = np.arange(16)[:, None]
    for t in range(VIS):
        J = (np.arange(N) + 1 + t % (N - 1)) % N
        filled = s >= 0
        old = np.take_along_axis(x, np.maximum(s, 0).reshape(N, 8, 1, 16 * LA), 3).reshape(N, 8, 16, 16, LA)
        m = np.minimum(z[:, :, :, None], old)
        free = filled & (np.add.reduce(m, axis=2) < np.add.reduce(old, axis=2))
        done = np.zeros((N, 8, LA), bool); best = z; put = np.zeros((N, 8, LA), np.int64)
        for trial in range(TRY):
            has = np.any(free, axis=2) & ~done; k = np.argmax(free, axis=2)
            cand = np.take_along_axis(m, k[:, :, None, None], 3)[:, :, :, 0]
            h = hashes(cand, w[J], p[J], t)[1]
            b = np.take_along_axis(c[J], h.reshape(N, 8, 1, 16 * LA), 3).reshape(N, 8, 16, 16, LA)
            met = np.add.reduce((b <= cand[:, :, :, None]).astype(np.int32), axis=2) >= R1
            neg = has & (np.add.reduce(met.astype(np.int32), axis=2) >= A[t] + bit[J][:, None])
            bit[J] = np.add.reduce(neg.astype(np.int64), axis=1) & 1
            best = np.where(neg[:, :, None], cand, best); put = np.where(neg, k, put); done = done | neg
            free = free & (k16 != k[:, :, None])
        put = np.where(done, put, np.where(np.any(~filled, axis=2), np.argmax(~filled, axis=2), t))
        n = SUB * np.arange(LA) + (hashes(best, w, p, t)[0] & (SUB - 1))
        near = filled & (np.add.reduce((old <= best[:, :, :, None]).astype(np.int32), axis=2) >= R2)
        v = np.maximum(best, np.maximum.reduce(np.where(near[:, :, None], old, 0), axis=3))
        h0 = hashes(v, w, p, t)[1][:, :, :1]
        z = np.abs(v - np.take_along_axis(c, h0, 3))
        np.put_along_axis(x, np.ascontiguousarray(np.broadcast_to(n[:, :, None], (N, 8, 16, LA))), best, 3)
        s = np.where(k16 == put[:, :, None], n[:, :, None], s)
    return {"yx": x.reshape(N, 128, W).astype(np.float32).astype(BF), "yl": s.reshape(N, 128, LA).astype(np.float32), "yz": z.reshape(N, 128, LA).astype(np.float32).astype(BF)}

@@ -1,0 +1,675 @@
+from concourse.bass import DstId, RemoteDMATransfer
+from concourse.mybir import dt, AluOpType, AxisListType, ActivationFunctionType
+
+OP = AluOpType
+AF = ActivationFunctionType
+VIS, NB = 5, 4096
+AT = [5, 4, 4, 3, 3]
+EXT = 4496
+CUT = 2304
+MG = 12582912.0
+KA = 8
+BIG = -8192.0
+
+SB = {"x": (1024, "bfloat16"), "ce": (EXT, "bfloat16"), "hb": (EXT, "bfloat16"), "sli": (128, "int32"), "zi": (128, "bfloat16"),
+      "wti": (1, "int32"), "kpi": (1, "int32"), "par": (8, "bfloat16"), "pr": (32, "bfloat16"),
+      "pi": (1, "int32"), "pg": (1, "int32"), "pq": (1, "int32"), "ji": (144, "int32"), "jg": (128, "int32"),
+      "pf": (1, "float32"), "pgf": (1, "float32"), "pqf": (1, "float32"), "pwf": (1, "float32"), "oh": (16, "float32"),
+      "w7": (1, "int32"), "wa": (1, "float32"), "w8": (1, "float32"), "cc": (1, "float32"), "ccb": (1, "float32"),
+      "bo": (128, "bfloat16"), "bo100": (128, "bfloat16"), "id": (128, "bfloat16"), "idn": (128, "bfloat16"), "id2": (128, "bfloat16"),
+      "id8": (128, "bfloat16"), "idh": (128, "bfloat16"), "ine": (128, "bfloat16"), "gt": (128, "bfloat16"), "lt": (128, "bfloat16"),
+      "ta": (128, "bfloat16"), "ts": (128, "bfloat16"), "tb": (128, "bfloat16"), "te": (128, "bfloat16"), "tc": (128, "bfloat16"),
+      "wd": (144, "bfloat16"), "wdf": (144, "bfloat16"), "wdw": (144, "bfloat16"), "wdh": (144, "float16"), "wds": (144, "float16"),
+      "ih": (128, "float16"), "ihn": (128, "float16"), "in8": (128, "float16"), "bm": (2048, "bfloat16"), "one": (128, "bfloat16"),
+      "ca": (128, "bfloat16"), "cb": (64, "bfloat16"), "cq": (64, "bfloat16"), "on32": (128, "bfloat16"), "on16": (128, "bfloat16"),
+      "jb": (128, "bfloat16"), "b8": (128, "bfloat16"), "b8x": (128, "bfloat16"), "thr": (1, "float32"), "tbc": (16, "float32"),
+      "k0": (1, "float32"), "kpb": (1, "bfloat16")}
+for _t in range(VIS):
+    SB["wq%d" % _t] = (128, "bfloat16")
+    SB["kc%d" % _t] = (1, "float32")
+    if _t:
+        SB["bk%d" % _t] = (NB, "bfloat16")
+for _h in range(2):
+    for _n, _w, _d in (("o0", 1024, "bfloat16"), ("o1", 1024, "bfloat16"), ("b", 2048, "bfloat16"), ("gg", 1024, "bfloat16"),
+                       ("gb", 2048, "bfloat16"), ("zz", 128, "bfloat16"), ("so", 64, "uint16"), ("sf", 64, "float16"),
+                       ("em", 64, "bfloat16"), ("op", 64, "bfloat16"), ("se", 128, "bfloat16"), ("ss", 128, "float16"),
+                       ("lo", 8, "uint16"), ("cd", 128, "bfloat16"), ("ci", 128, "bfloat16"), ("gi", 128, "bfloat16"), ("rc", 128, "bfloat16"), ("qb", 128, "bfloat16"),
+                       ("ww", 128, "float32"), ("y", 128, "int32"), ("y2", 128, "int32"), ("ho", 128, "uint16"),
+                       ("ge", 128, "bfloat16"), ("rg", 128, "bfloat16"), ("ng", 128, "bfloat16"), ("qn", 64, "bfloat16"),
+                       ("qn2", 64, "bfloat16"), ("d", 64, "bfloat16"), ("pp", 128, "bfloat16"), ("mp", 128, "bfloat16"),
+                       ("m", 64, "bfloat16"), ("pm", 64, "bfloat16"), ("qf", 64, "float16"), ("ns", 64, "float16"),
+                       ("tt", 64, "float16"), ("no", 8, "uint16"), ("nn", 64, "bfloat16"), ("ac", 128, "bfloat16"),
+                       ("c0", 64, "bfloat16"), ("c", 64, "bfloat16"), ("ui", 4, "int32"), ("uj", 4, "int32"), ("uw", 4, "float32"),
+                       ("uy", 4, "int32"), ("uz", 4, "int32"), ("co", 8, "uint16"), ("df", 64, "bfloat16"), ("yl", 64, "float32")):
+        SB["%s_%d" % (_n, _h)] = (_w, _d)
+    for _t in range(1, VIS):
+        SB["bs%d_%d" % (_t, _h)] = (64, "bfloat16")
+        SB["rb%d_%d" % (_t, _h)] = (64, "bfloat16")
+
+
+def _pack():
+    place, scratch, fill = {}, {}, {}
+    for n in sorted(SB):
+        w, d = SB[n]
+        if w >= 1024:
+            scratch["s_" + n] = ("sbuf", [128, w], d)
+            place[n] = ("s_" + n, 0, d)
+        else:
+            step = (w + 15) // 16 * 16
+            place[n] = ("k_" + d, fill.setdefault(d, 0), d)
+            fill[d] += step
+    for d in fill:
+        scratch["k_" + d] = ("sbuf", [128, fill[d]], d)
+    for h in range(2):
+        for p in ("pz", "pn", "ps", "pd"):
+            n = "%s_%d" % (p, h)
+            scratch[n] = ("psum", [128, 512], "float32")
+            place[n] = (n, 0, "float32")
+    return place, scratch
+
+
+PLACE, SCRATCH = _pack()
+DMAS = 16
+SEMAPHORES = (["sv", "sa", "st", "sg", "ls", "hb0", "hb1", "pr", "bk1", "bk2", "bk3", "bk4", "rc0", "rc1", "rg0", "rg1"]
+              + ["rb%d_%d" % (t, h) for t in range(1, VIS) for h in range(2)] + ["dm%d" % i for i in range(DMAS)])
+CYC = 0.00104
+PEC = 0.00052
+HOP = 0.06
+MSG = 3.5
+BIAS = 4.0
+PREF = {}
+GC = 1.56
+VO = (16, 16)
+VB = (16, 16, 16, 16)
+ORDER = {}
+
+
+def helpers(T, topo, r):
+    n = len(T.cores)
+    own = T.cores[r]
+    out = []
+    for same, ts in ((True, (1, 3)), (False, (2, 4))):
+        for c in topo.cores_of(own):
+            if c != own and (topo.die(c) == topo.die(own)) == same and all(topo.may_write(c, T.cores[(r - 1 - t) % n]) for t in ts):
+                out.append((c, ts))
+                break
+    return out
+
+
+def pieces(t):
+    return ((97 * t, CUT), (CUT, 97 * t + NB))
+
+
+def forward(g, core, T, topo, r, ts):
+    n = len(T.cores)
+    hb, sent = T[PLACE["hb"][0]], 0
+    for t in ts:
+        dst = T.cores[(r - 1 - t) % n]
+        rid, pid = topo.addr(dst, core)
+        for i, (a, b) in enumerate(pieces(t)):
+            if t == ts[0]:
+                g.wait_ge(T.sem["hb%d" % i], len(onchip(T, topo, r, core)))
+            g.remote_dma(out_ap=T["s_bk%d" % t][:, a - 97 * t:b - 97 * t], in_ap=hb[:, a:b], remote_sem=T.sem["bk%d" % t],
+                         local_sem=T.sem.ls, pid=pid, routing_id=rid, dma_engine_mask=topo.mask(core, dst))
+            sent += len(topo.engines(core, dst))
+    g.wait_ge(T.sem.ls, sent)
+
+
+def onchip(T, topo, r, helper):
+    n = len(T.cores)
+    own = T.cores[r]
+    off = topo.engines(own, T.cores[(r + 1) % n])
+    return [e for e in topo.engines(own, helper) if e not in off]
+
+
+def rank_program(g, core, T, topo):
+    n = len(T.cores)
+    rank = T.rank_of(core)
+    if rank is None:
+        for r in range(n):
+            for c, ts in helpers(T, topo, r):
+                if c == core:
+                    forward(g, core, T, topo, r, ts)
+        return
+    ops = []
+    hist, banks = {}, {}
+    ndma, local, cur = [0], [0], ["-"]
+    QUEUE = {"V": g.vector, "A": g.scalar, "T": g.tensor, "G": g, "S": g.sync}
+    KEY = {"V": "sv", "A": "sa", "T": "st", "G": "sg"}
+
+    def ap(x):
+        name, a, b = x[0], x[1], x[2]
+        if name in PLACE:
+            buf, off, _d = PLACE[name]
+            if len(x) > 3:
+                return T[buf][:, off + a:off + b:x[3]]
+            return T[buf][:, off + a:off + b]
+        return T[name][:, a:b]
+
+    def W(name, a=0, b=None):
+        return (name, a, SB[name][0] if b is None else b)
+
+    def psum(x):
+        return x[0] not in SB and x[0] in PLACE
+
+    def add(q, cost, fn, r=(), w=(), key=None, amount=1, release=0.0, extra=()):
+        i = len(ops)
+        deps = set(extra)
+        for items, wr in ((r, False), (w, True)):
+            for x in items:
+                if psum(x):
+                    e = banks.setdefault(x[0], [(None, []), (None, [])])
+                    if e[1][0] != q:
+                        e[0], e[1] = e[1], (q, [])
+                    deps.update(e[0][1])
+                    if q == "T":
+                        deps.update(e[1][1][-1:])
+                    e[1][1].append(i)
+                elif x[0] in SB:
+                    for (a, e, j, jw) in hist.setdefault(x[0], []):
+                        if a < x[2] and x[1] < e and (wr or jw):
+                            deps.add(j)
+        for x in r:
+            if x[0] in SB:
+                hist[x[0]].append((x[1], x[2], i, False))
+        for x in w:
+            if x[0] in SB:
+                hist[x[0]] = [y for y in hist[x[0]] if not (x[1] <= y[0] and y[1] <= x[2])] + [(x[1], x[2], i, True)]
+        deps.discard(i)
+        ops.append([q, KEY.get(q) if key is None else key, amount, fn, cost, sorted(deps), release, bias(r, w)])
+        return i
+
+    def bias(r, w):
+        h = 0 if any(x[0].endswith("_0") for x in list(r) + list(w)) else 1
+        return PREF.get(cur[0] + str(h), 0.0) + (BIAS if h == 0 else 0.0)
+
+    def width(x):
+        return (x[2] - x[1] + (x[3] if len(x) > 3 else 1) - 1) // (x[3] if len(x) > 3 else 1)
+
+    def half(*xs):
+        return all(not psum(x) and PLACE[x[0]][2] in ("bfloat16", "float16", "uint16") for x in xs)
+
+    def vcost(cyc):
+        return CYC * max(64, cyc)
+
+    def isap(s):
+        return isinstance(s, tuple)
+
+    def val(s):
+        return ap(s) if isap(s) else s
+
+    def tt(out, a, b, op):
+        c = width(out) * (1 if psum(a) or psum(b) else 2)
+        return add("V", vcost(c), lambda: g.vector.tensor_tensor(ap(out), ap(a), ap(b), op), [a, b], [out])
+
+    def ts(out, a, s1, op0, s2=None, op1=None):
+        c = width(out) * (0.5 if half(out, a) else 1)
+        rd = [a] + [s for s in (s1, s2) if isap(s)]
+        if op1 is None:
+            return add("V", vcost(c), lambda: g.vector.tensor_scalar(ap(out), ap(a), val(s1), None, op0), rd, [out])
+        return add("V", vcost(c), lambda: g.vector.tensor_scalar(ap(out), ap(a), val(s1), val(s2), op0, op1), rd, [out])
+
+    def cp(out, a):
+        c = width(out) * (0.5 if half(out, a) else 1)
+        return add("V", vcost(c), lambda: g.vector.tensor_copy(ap(out), ap(a)), [a], [out])
+
+    def fill(out, v):
+        return add("V", vcost(width(out) * 0.5), lambda: g.vector.memset(ap(out), v), [], [out])
+
+    def act(out, a, func, bias=0.0, scale=1.0):
+        rd = [a] + ([bias] if isap(bias) else [])
+        return add("A", vcost(width(out)), lambda: g.scalar.activation(ap(out), ap(a), func, bias=val(bias), scale=scale), rd, [out])
+
+    def agather(out, win, off, share):
+        for q, a, b in (("V", 64 - share, 64), ("A", 0, 64 - share)):
+            if a == b:
+                continue
+            o, f = (out[0], out[1] + 16 * a, out[1] + 16 * b), (off[0], off[1] + a, off[1] + b)
+
+            def fn(q=q, o=o, f=f):
+                if q == "V":
+                    return g.vector.tensor_copy(ap(o), ap(win).indirect(ap(f)))
+                return g.scalar.activation(ap(o), ap(win).indirect(ap(f)), AF.Copy)
+            add(q, 0.06 + GC * CYC * width(o), fn, [win, f], [o])
+
+    def vgather(out, win, off, b, op):
+        return add("V", 0.05 + 1.56 * CYC * width(out),
+                   lambda: g.vector.tensor_tensor(ap(out), ap(win).indirect(ap(off)), ap(b), op), [win, off, b], [out])
+
+    def scatter(win, off, a):
+        return add("V", 0.05 + 3.8 * CYC * width(a), lambda: g.vector.tensor_copy(ap(win).indirect(ap(off)), ap(a)), [off, a], [win])
+
+    def mms(out, pairs):
+        for j in range(len(pairs)):
+            l, r = pairs[j]
+
+            def fn(l=l, r=r, s=j == 0, e=j == len(pairs) - 1):
+                return g.tensor.matmul(ap(out), ap(l), ap(r), s, e)
+            add("T", PEC * max(64, width(out)), fn, [l, r], [out])
+
+    def dma(out, a, cost=2.0):
+        s = "dm%d" % ndma[0]
+        ndma[0] += 1
+        return add("S", cost, lambda: g.sync.dma_start(ap(out), ap(a)), [a], [out], key=s, amount=16)
+
+    def send(dst, out, a, sem):
+        rid, pid = topo.addr(dst, core)
+        mask = topo.mask(core, dst)
+        local[0] += len(topo.engines(core, dst))
+
+        def fn():
+            g.remote_dma(out_ap=ap(out), in_ap=ap(a), remote_sem=T.sem[sem], local_sem=T.sem.ls, pid=pid, routing_id=rid,
+                         dma_engine_mask=mask)
+        return add("G", 1.0, fn, [a], [], key="")
+
+    def arrive(buf, sem, total, after=None, wait=0.0, release=0.0):
+        add("X", wait, None, [], [buf], key=sem, amount=total, release=release, extra=() if after is None else (after,))
+
+    def R(m, r):
+        return (m, 15 - r, 143 - r)
+
+    prev1 = T.cores[(rank - 1) % n]
+    next1 = T.cores[(rank + 1) % n]
+
+    dma(W("sli"), ("sl", 0, 128))
+    dma(W("x"), ("x0", 0, 1024), 3.0)
+    dma(W("zi"), ("z0", 0, 128))
+    dma(W("wti"), ("wt", 0, 1))
+    dma(W("kpi"), ("kp", 0, 1))
+    dma(W("ce", 0, CUT), ("cl", 0, CUT), 4.0)
+    dma(W("ce", CUT, NB), ("cl", CUT, NB), 4.0)
+    dma(W("ce", NB, EXT), ("cl", 0, EXT - NB), 2.0)
+
+    add("G", 0.14, lambda: g.iota(ap(W("pi")), [[0, 1]], 0, 1), [], [W("pi")])
+    add("G", 0.4, lambda: g.iota(ap(W("ji")), [[1, 144]], 0, 0), [], [W("ji")])
+    J128 = W("ji", 0, 128)
+    cp(W("pf"), W("pi"))
+    ts(W("pg"), W("pi"), 4, OP.arith_shift_right)
+    ts(W("pq"), W("pi"), 15, OP.bitwise_and)
+    cp(W("pgf"), W("pg"))
+    cp(W("pqf"), W("pq"))
+    ts(W("jg"), J128, 4, OP.arith_shift_right)
+    ts(W("pwf"), W("pg"), 16.0, OP.mult, 15.0, OP.add)
+    ts(W("id"), J128, W("pf"), OP.is_equal)
+    ts(W("ih"), W("id"), 1.0, OP.mult)
+    ts(W("idn"), W("id"), -1.0, OP.mult)
+    ts(W("bo"), W("jg"), W("pgf"), OP.is_equal)
+    ts(W("wd"), W("ji"), W("pwf"), OP.is_equal)
+    ts(W("oh"), W("ji", 0, 16), W("pqf"), OP.is_equal)
+    ts(W("ine"), W("id"), BIG, OP.mult)
+    ts(W("gt"), J128, W("pf"), OP.is_gt)
+    tt(W("lt"), W("gt"), W("bo"), OP.mult)
+    ts(W("ta"), W("id"), -100.0, OP.mult)
+    tt(W("ts"), W("ta"), W("lt"), OP.add)
+    ts(W("wdh"), W("wd"), 1.0, OP.mult)
+    fill(W("par"), 0.0)
+    cp(W("par", 0, 1), W("wti"))
+    cp(W("par", 1, 2), W("kpi"))
+    fill(W("one"), 1.0)
+    ts(W("cc"), W("oh", 0, 1), -0.5, OP.mult)
+    ts(W("ccb"), W("oh", 1, 2), 2.0 ** -13, OP.mult)
+    tt(W("cc"), W("cc"), W("ccb"), OP.add)
+    ts(W("ca"), W("one"), W("cc"), OP.mult)
+
+    def weights(t, src, c):
+        ts(W("wq%d" % t), W("bo"), (src, c, c + 1), OP.mult, 2.0 ** -12, OP.mult)
+        ts(W("kc%d" % t), (src, c + 1, c + 2), 2.0 ** 17, OP.mult)
+    weights(0, "par", 0)
+    ts(W("id2"), W("id"), 2.0, OP.mult)
+    ts(W("id8"), W("id"), 8.0, OP.mult)
+    ts(W("idh"), W("id"), -100.0, OP.mult)
+    ts(W("bo100"), W("bo"), 100.0, OP.mult)
+    ts(W("tb"), W("id"), -8.0, OP.mult)
+    ts(W("tc"), W("lt"), 8.0, OP.mult)
+    tt(W("te"), W("tb"), W("tc"), OP.add)
+    ts(W("wdf"), W("wd"), 0.5, OP.mult)
+    ts(W("wds"), W("wd"), 1.0 / 16, OP.mult)
+    ts(W("ihn"), W("id"), -1.0, OP.mult)
+    ts(W("in8"), W("id"), -8.0, OP.mult)
+    ts(W("tbc"), W("oh"), -1.0, OP.mult)
+    ts(W("cb"), W("one", 0, 64), W("oh", 0, 1), OP.mult, -0.25, OP.mult)
+    ts(W("cq"), W("one", 0, 64), W("oh", 0, 1), OP.mult, -7.0 / 16, OP.mult)
+    fill(W("on32"), 1.0 / 32)
+    fill(W("on16"), -1.0 / 16)
+    cp(W("jb"), J128)
+    ts(W("thr"), W("pqf"), KA - 0.5, OP.is_ge, -8.0, OP.mult)
+    ts(W("thr"), W("thr"), 11.5, OP.add)
+    ts(W("w7"), W("wti"), 7, OP.bitwise_and)
+    ts(W("wa"), W("w7"), 3.5, OP.is_ge, -8.0, OP.mult)
+    tt(W("w8"), W("wa"), W("w7"), OP.add)
+    ts(W("b8"), W("bo"), W("w8"), OP.mult, 0.125, OP.mult)
+    ts(W("b8x"), W("bo"), W("w8"), OP.mult)
+    ts(W("wdw"), W("wd"), W("par", 0, 1), OP.mult)
+    for k in range(16):
+        ts(W("bm", 128 * k, 128 * k + 128), W("bo"), W("oh", k, k + 1), OP.mult, -512.0, OP.mult)
+    cp(W("kpb"), W("kpi"))
+    mms(("ps_0", 72, 73), [(W("bm", 0, 128), W("kpb"))])
+    ts(W("k0"), ("ps_0", 72, 73), -32.0 / 512, OP.mult)
+
+    def params(after):
+        add("G", 2.0, fused, [W("par")], [], key="", extra=[after])
+        local[0] += nsm
+
+    def fused():
+        dsts = [T.cores[(rank - 1 - t) % n] for t in range(1, VIS)]
+        ids = []
+        for d in dsts:
+            rid, pid = topo.addr(d, core)
+            ids.append(DstId(rid=rid, pnc=pid))
+        outs = [ap(W("pr", 8 * t - 8, 8 * t)) for t in range(1, VIS)]
+        g.remote_dma_fused([RemoteDMATransfer(dst_ids=ids, dma_engine_mask=topo.mask(core, dsts[0]), remote_sem=T.sem.pr,
+                                              srcs=[ap(W("par"))], dsts=outs)], local_sem=T.sem.ls)
+    nsm = len(topo.engines(core, prev1))
+    arrive(W("pr"), "pr", nsm * (VIS - 1), release=12.0)
+
+    def book(i, a, b, after):
+        def fn():
+            for c, _ts in helpers(T, topo, rank):
+                rid, pid = topo.addr(c, core)
+                e = onchip(T, topo, rank, c)
+                g.remote_dma(out_ap=ap(W("hb", a, b)), in_ap=ap(W("ce", a, b)), remote_sem=T.sem["hb%d" % i], local_sem=T.sem.ls,
+                             pid=pid, routing_id=rid, dma_engine_mask=sum(1 << x for x in e))
+        add("G", 2.0, fn, [W("ce", a, b)], [], key="", extra=[after])
+        local[0] += sum(len(onchip(T, topo, rank, c)) for c, _ts in helpers(T, topo, rank))
+    for t in range(1, VIS):
+        arrive(W("bk%d" % t), "bk%d" % t, 2 * nsm, release=(0, 22.0, 24.0, 32.0, 34.0)[t])
+
+    HV = range(2)
+    for h in HV:
+        s = "_%d" % h
+        a, b = 64 * h, 64 * h + 64
+        cp(W("sf" + s), W("sli", a, b))
+        mms(("ps" + s, 80, 144), [(W("ih"), W("sf" + s))])
+        act(W("zz" + s, 0, 64), W("zi", a, b), AF.Copy)
+        act(W("zz" + s, 64, 128), W("zi", a, b), AF.Copy)
+        mms(("pz" + s, 0, 64), [(W("id"), W("zz" + s, 0, 64))])
+
+    def slots_in(s, first):
+        SP = ("ps" + s, 80, 144)
+        cp(W("so" + s), SP)
+        ts(W("em" + s), SP, -0.5, OP.is_lt)
+        if not first:
+            cp(W("sf" + s), SP)
+
+    for h in HV:
+        slots_in("_%d" % h, True)
+    for t in range(VIS):
+        CD, GE = ("cd", "ge") if t else ("ci", "gi")
+        cur[0] = "g"
+        for h in HV:
+            s = "_%d" % h
+            agather(W("o%d" % (t % 2) + s), W("x"), W("so" + s), VO[h])
+        cur[0] = "d"
+        for h in HV:
+            s = "_%d" % h
+            mms(("ps" + s, 0, 64), [(W("te"), W("em" + s)), (R("wdf", t), W("em" + s))])
+            ts(W("d" + s), ("ps" + s, 0, 64), W("tbc", t, t + 1), OP.add, -0.9, OP.is_le)
+        cur[0] = "o"
+        for h in HV:
+            s = "_%d" % h
+            o, gg = "o%d" % (t % 2) + s, "gg" + s
+            for k in range(KA, 16):
+                c = 64 * (k - KA)
+                mms(("pd" + s, c, c + 64), [(W("id"), (o, k, 1024, 16)), (W("idn"), W("zz" + s, 0, 64))])
+            act(W(gg, 64 * KA, 1024), ("pd" + s, 0, 64 * (16 - KA)), AF.Relu)
+            for k in range(KA):
+                tt(W(gg, 64 * k, 64 * k + 64), (o, k, 1024, 16), ("pz" + s, 0, 64), OP.is_gt)
+            mms(("pn" + s, 0, 64), [(W("ine"), W("em" + s))] + [(R("wd", k), W(gg, 64 * k, 64 * k + 64)) for k in range(16)])
+            ts(W("op" + s), ("pn" + s, 0, 64), 0.5, OP.is_gt)
+        cur[0] = "s"
+        for h in HV:
+            s = "_%d" % h
+            mms(("ps" + s, 0, 64), [(W("ts"), W("op" + s))])
+            for j in range(2):
+                c = 64 * j
+                ts(W("se" + s, c, c + 64), ("ps" + s, 0, 64), -100.0 + j, OP.is_equal)
+                tt(W("ss" + s, c, c + 64), W("se" + s, c, c + 64), ("ps" + s, 80, 144), OP.mult)
+            mms(("ps" + s, 64, 72), [(R("wdh", r), ("ss" + s, r, 128, 16)) for r in range(16)])
+            cp(W("lo" + s), ("ps" + s, 64, 72))
+            vgather(W(CD + s), W("x"), W("lo" + s), W("zz" + s), OP.min)
+            if t == 0:
+                i = send(next1, W("rc" + s), W(CD + s), "rc%d" % h)
+                arrive(W("rc" + s), "rc%d" % h, nsm, after=i, wait=MSG)
+        if t == 0:
+            book(0, 0, CUT, i)
+            book(1, CUT, EXT, i)
+            params(i)
+        cur[0] = "h"
+        for h in HV:
+            s = "_%d" % h
+            cs = W(("cd" if t else "rc") + s)
+            wq = W("wq%d" % t)
+            if t and h == 0:
+                weights(t, "pr", 8 * t - 8)
+            mms(("ps" + s, 144, 272), [(W("bo"), W("ca")), (wq, cs)])
+            ts(W("qb" + s), ("ps" + s, 144, 272), MG, OP.add, MG, OP.subtract)
+            mms(("ps" + s, 272, 400), [(wq, cs), (W("idn"), W("qb" + s))])
+            mms(("pz" + s, 64, 192), [(W("id"), cs)])
+            act(W("ww" + s), ("ps" + s, 272, 400), AF.Identity, bias=W("kc%d" % t), scale=2.0 ** 24)
+            tt(W("y" + s), W("ww" + s), ("ps" + s, 272, 400), OP.mult)
+            ts(W("y2" + s), W("y" + s), 5, OP.arith_shift_right, 4095, OP.bitwise_and)
+            cp(W("ho" + s), W("y2" + s))
+        cur[0] = "b"
+        for h in HV:
+            s = "_%d" % h
+            win = W("bk%d" % t) if t else W("ce", 0, NB)
+            for j in range(2):
+                c = 64 * j
+                agather(W("b" + s, 1024 * j, 1024 * j + 1024), win, W("ho" + s, c, c + 64), VB[2 * h + j])
+                for m in range(16):
+                    e = 1024 * j + 64 * m
+                    tt(W("gb" + s, e, e + 64), ("b" + s, 1024 * j + m, 1024 * j + 1024, 16), ("pz" + s, 64 + c, 128 + c), OP.is_le)
+                mms(("pn" + s, 64 + c, 128 + c), [(R("wd", m), W("gb" + s, 1024 * j + 64 * m, 1024 * j + 64 * m + 64)) for m in range(16)])
+                ts(W(GE + s, c, c + 64), ("pn" + s, 64 + c, 128 + c), 8.5, OP.is_ge)
+            if t == 0:
+                i = send(prev1, W("rg" + s), W(GE + s), "rg%d" % h)
+                arrive(W("rg" + s), "rg%d" % h, nsm, after=i, wait=MSG)
+        cur[0] = "v"
+        for h in HV:
+            s = "_%d" % h
+            PS = "ps" + s
+            ge, se, ng = ("ge" if t else "rg") + s, "se" + s, "ng" + s
+            thr = 99.5 + AT[t]
+            zz = W("zz" + s, 0, 64)
+            mms((PS, 144, 272), [(W("id"), W(CD + s)), (W("idn"), W("zz" + s))])
+            mms((PS, 272, 336), [(W("id"), W(se, 0, 64)), (W("idn"), W("d" + s))])
+            mms((PS, 336, 400), [(W("id"), W(se, 64, 128)), (W("idn"), W("d" + s))])
+            bits = [(W("id"), W("rb%d" % t + s))] if t else []
+            mms((PS, 0, 64), [(W("bo100"), W(se, 0, 64)), (W("bo"), W(ge, 0, 64))] + bits)
+            ts(W(ng, 0, 64), (PS, 0, 64), thr, OP.is_ge)
+            mms((PS, 400, 464), [(W("bo"), W("cb")), (W("on32"), W(ng, 0, 64))])
+            ts(W("qn" + s), (PS, 400, 464), MG, OP.add, MG, OP.subtract)
+            mms((PS, 0, 64), [(W("bo100"), W(se, 64, 128)), (W("bo"), W(ge, 64, 128)), (W("idh"), W(ng, 0, 64)), (W("on16"), W(ng, 0, 64)),
+                              (W("id2"), W("qn" + s))])
+            ts(W(ng, 64, 128), (PS, 0, 64), thr, OP.is_ge)
+            for j in range(2):
+                c = 64 * j
+                tt(W("pp" + s, c, c + 64), W(ng, c, c + 64), (PS, 144 + c, 208 + c), OP.mult)
+                tt(W("mp" + s, c, c + 64), W(ng, c, c + 64), (PS, 272 + c, 336 + c), OP.mult)
+            mms(("pz" + s, 192, 256), [(W("id"), zz), (W("id"), W("pp" + s, 0, 64)), (W("id"), W("pp" + s, 64, 128))])
+            cp(W("m" + s), ("pz" + s, 192, 256))
+        cur[0] = "n"
+        for h in HV:
+            s = "_%d" % h
+            PS = "ps" + s
+            parts = [W("zz" + s, 0, 64), W("pp" + s, 0, 64), W("pp" + s, 64, 128)]
+            mms((PS, 208, 272), [(W("bo"), W("cq"))] + [(W("b8"), x) for x in parts])
+            ts(W("qf" + s), (PS, 208, 272), MG, OP.add, MG, OP.subtract)
+            mms((PS, 144, 208), [(W("id"), W("d" + s)), (W("id"), W("mp" + s, 0, 64)), (W("id"), W("mp" + s, 64, 128))])
+            cp(W("pm" + s), (PS, 144, 208))
+            mms((PS, 272, 336), [(W("b8x"), x) for x in parts]
+                + [(W("id8"), W("jb", 64 * h, 64 * h + 64)), (W("in8"), W("qf" + s))])
+            cp(W("ns" + s), (PS, 272, 336))
+            mms(("pn" + s, 192, 196), [(R("wds", r), ("ns" + s, r, 64, 16)) for r in range(16)])
+            cp(W("no" + s, 0, 4), ("pn" + s, 192, 196))
+            scatter(W("x"), W("no" + s, 0, 4), W("m" + s))
+            mms((PS, 336, 400), [(W("ih"), W("ns" + s)), (W("ihn"), W("sf" + s))])
+            tt(W("tt" + s), W("pm" + s), (PS, 336, 400), OP.mult)
+            mms((PS, 80, 144), [(W("ih"), W("sf" + s)), (W("ih"), W("tt" + s))])
+        cur[0] = "j"
+        if t < VIS - 1:
+            for h in HV:
+                s = "_%d" % h
+                PS, ng = "ps" + s, "ng" + s
+                mms((PS, 400, 464), [(W("bo"), W("cb")), (W("on32"), W(ng, 64, 128))])
+                ts(W("qn2" + s), (PS, 400, 464), MG, OP.add, MG, OP.subtract)
+                mms((PS, 0, 64), [(W("on16"), W(ng, 64, 128)), (W("id2"), W("qn2" + s))])
+                act(W("bs%d" % (t + 1) + s), (PS, 0, 64), AF.Copy)
+                i = send(prev1, W("rb%d" % (t + 1) + s), W("bs%d" % (t + 1) + s), "rb%d" % (t + 1) + s)
+                arrive(W("rb%d" % (t + 1) + s), "rb%d" % (t + 1) + s, nsm, after=i, wait=MSG)
+        cur[0] = "r"
+        for h in HV:
+            s = "_%d" % h
+            o, gg = "o%d" % (t % 2) + s, "gg" + s
+            for k in range(KA, 16):
+                c = 64 * (k - KA)
+                mms(("pd" + s, c, c + 64), [(W("idn"), (o, k, 1024, 16)), (W("id"), W("m" + s))])
+            act(W(gg, 64 * KA, 1024), ("pd" + s, 0, 64 * (16 - KA)), AF.Sign, bias=0.5)
+            for k in range(KA):
+                tt(W(gg, 64 * k, 64 * k + 64), (o, k, 1024, 16), ("pz" + s, 192, 256), OP.is_le)
+            mms(("pn" + s, 0, 64), [(W("ine"), W("em" + s))]
+                + [(R("wd" if k < KA else "wdf", k), W(gg, 64 * k, 64 * k + 64)) for k in range(16)])
+            ts(W("nn" + s), ("pn" + s, 0, 64), W("thr"), OP.is_lt)
+        cur[0] = "i"
+        for h in HV:
+            s = "_%d" % h
+            if t < VIS - 1:
+                slots_in(s, False)
+            else:
+                cp(W("yl" + s), ("ps" + s, 80, 144))
+                dma(("yl", 64 * h, 64 * h + 64), W("yl" + s))
+        if t == VIS - 1:
+            dma(("yx", 0, 1024), W("x"))
+        cur[0] = "c"
+        for h in HV:
+            s = "_%d" % h
+            o = "o%d" % (t % 2) + s
+            for k in range(16):
+                p = ("pd" if k < 8 else "pn") + s
+                c = 64 * (k % 8)
+                mms((p, c, c + 64), [(W("id"), (o, k, 1024, 16)), (W("bm", 128 * k, 128 * k + 128), W("nn" + s))])
+            for k in range(0, 16, 2):
+                p = ("pd" if k < 8 else "pn") + s
+                c = 64 * (k % 8)
+                if k == 0:
+                    ts(W("ac" + s), (p, c, c + 128), 0.0, OP.max)
+                else:
+                    tt(W("ac" + s), W("ac" + s), (p, c, c + 128), OP.max)
+            tt(W("c0" + s), W("ac" + s, 0, 64), ("pz" + s, 192, 256), OP.max)
+            tt(W("c" + s), W("ac" + s, 64, 128), W("c0" + s), OP.max)
+        cur[0] = "z"
+        for h in HV:
+            s = "_%d" % h
+            PS = "ps" + s
+            mms((PS, 64, 68), [(R("wdw", r), ("c" + s, r, 64, 16)) for r in range(16)])
+            cp(W("ui" + s), (PS, 64, 68))
+            ts(W("uj" + s), W("ui" + s), 4095, OP.bitwise_and)
+            ts(W("uw" + s), W("uj" + s), W("k0"), OP.add)
+            tt(W("uy" + s), W("uw" + s), W("uj" + s), OP.mult)
+            ts(W("uz" + s), W("uy" + s), 5, OP.arith_shift_right, 4095, OP.bitwise_and)
+            ts(W("co" + s, 0, 4), W("uz" + s), 97.0 * t, OP.add)
+            vgather(W("df" + s), W("ce"), W("co" + s, 0, 4), W("c" + s), OP.subtract)
+            act(W("zz" + s, 0, 64), W("df" + s), AF.Abs)
+            if t < VIS - 1:
+                mms(("pz" + s, 0, 64), [(W("id"), W("zz" + s, 0, 64))])
+                act(W("zz" + s, 64, 128), W("df" + s), AF.Abs)
+            else:
+                dma(("yz", 64 * h, 64 * h + 64), W("zz" + s, 0, 64))
+
+    if "order" not in ORDER:
+        ORDER["order"] = schedule(ops)
+    known = {q: {} for q in QUEUE}
+    count, clock = {}, {}
+    for i in ORDER["order"]:
+        q, key, amount, fn, _c, deps, _r, _b = ops[i]
+        if q == "X":
+            clock[i] = {key: amount}
+            count[key] = amount
+            continue
+        k = known[q]
+        need = {}
+        for d in deps:
+            if ops[d][0] == "T" and q == "T":
+                continue
+            kd = ops[d][1]
+            if kd == "" or kd is None:
+                continue
+            v = clock[d][kd]
+            if k.get(kd, 0) < v and need.get(kd, (0, 0))[0] < v:
+                need[kd] = (v, d)
+        for kd in list(need):
+            v, d = need[kd]
+            for k2 in need:
+                if k2 != kd and clock[need[k2][1]].get(kd, 0) >= v:
+                    del need[kd]
+                    break
+        for kd in need:
+            v, d = need[kd]
+            QUEUE[q].wait_ge(T.sem[kd], v)
+            for kk in clock[d]:
+                if k.get(kk, 0) < clock[d][kk]:
+                    k[kk] = clock[d][kk]
+        ins = fn()
+        c = dict(k)
+        if key:
+            count[key] = count.get(key, 0) + amount
+            ins.then_inc(T.sem[key], amount)
+            c[key] = count[key]
+        clock[i] = c
+    for key in sorted(count):
+        g.wait_ge(T.sem[key], count[key])
+    g.wait_ge(T.sem.ls, local[0])
+
+
+def schedule(ops):
+    m = len(ops)
+    users = [[] for _ in range(m)]
+    left = [0] * m
+    for i in range(m):
+        for d in ops[i][5]:
+            users[d].append(i)
+            left[i] += 1
+    tail = [0.0] * m
+    for i in range(m - 1, -1, -1):
+        tail[i] = ops[i][4] + max([HOP + tail[u] for u in users[i]] + [0.0])
+    free = {"V": 0.0, "A": 0.0, "T": 0.0, "G": 0.0, "S": 0.0}
+    ready = {q: [] for q in free}
+    est = [ops[i][6] for i in range(m)]
+    order, start = [], [0.0] * m
+    work = [i for i in range(m) if left[i] == 0]
+
+    def done(i, end):
+        for u in users[i]:
+            est[u] = max(est[u], end + (0.0 if ops[i][0] == "T" and ops[u][0] == "T" else HOP))
+            left[u] -= 1
+            if left[u] == 0:
+                work.append(u)
+
+    while True:
+        while work:
+            i = work.pop()
+            if ops[i][0] == "X":
+                start[i] = est[i]
+                order.append(i)
+                done(i, est[i] + ops[i][4])
+            else:
+                ready[ops[i][0]].append(i)
+        best = None
+        for q in ready:
+            if ready[q]:
+                t0 = max(free[q], min(est[i] for i in ready[q]))
+                if best is None or t0 < best[0]:
+                    best = (t0, q)
+        if best is None:
+            break
+        t0, q = best
+        i = max((j for j in ready[q] if est[j] <= t0), key=lambda j: (tail[j] + ops[j][7], -j))
+        ready[q].remove(i)
+        start[i] = t0
+        order.append(i)
+        end = t0 + ops[i][4]
+        free[q] = t0 + (0.1 if q == "S" else ops[i][4])
+        done(i, end)
+    ORDER["span"] = max(start[i] + ops[i][4] for i in range(m))
+    ORDER["start"] = start
+    return order

@@ -8,7 +8,7 @@ AT = [5, 4, 4, 3, 3]
 EXT = 4496
 CUT = 2304
 MG = 12582912.0
-KA = 8
+KA = 16
 BIG = -8192.0
 
 SB = {"x": (1024, "bfloat16"), "ce": (EXT, "bfloat16"), "hb": (EXT, "bfloat16"), "sli": (128, "int32"), "zi": (128, "bfloat16"),
@@ -19,7 +19,8 @@ SB = {"x": (1024, "bfloat16"), "ce": (EXT, "bfloat16"), "hb": (EXT, "bfloat16"),
       "bo": (128, "bfloat16"), "bo100": (128, "bfloat16"), "id": (128, "bfloat16"), "idn": (128, "bfloat16"), "id2": (128, "bfloat16"),
       "id8": (128, "bfloat16"), "idh": (128, "bfloat16"), "ine": (128, "bfloat16"), "gt": (128, "bfloat16"), "lt": (128, "bfloat16"),
       "ta": (128, "bfloat16"), "ts": (128, "bfloat16"), "tb": (128, "bfloat16"), "te": (128, "bfloat16"), "tc": (128, "bfloat16"),
-      "wd": (144, "bfloat16"), "wdf": (144, "bfloat16"), "wdw": (144, "bfloat16"), "wdh": (144, "float16"), "wds": (144, "float16"),
+      "wd": (144, "bfloat16"), "wdf": (144, "bfloat16"), "bow": (128, "bfloat16"), "boh": (128, "float16"), "dg": (128, "bfloat16"),
+      "rs": (128, "bfloat16"),
       "ih": (128, "float16"), "ihn": (128, "float16"), "in8": (128, "float16"), "bm": (2048, "bfloat16"), "one": (128, "bfloat16"),
       "ca": (128, "bfloat16"), "cb": (64, "bfloat16"), "cq": (64, "bfloat16"), "on32": (128, "bfloat16"), "on16": (128, "bfloat16"),
       "jb": (128, "bfloat16"), "b8": (128, "bfloat16"), "b8x": (128, "bfloat16"), "thr": (1, "float32"), "tbc": (16, "float32"),
@@ -37,7 +38,7 @@ for _h in range(2):
                        ("ww", 128, "float32"), ("y", 128, "int32"), ("y2", 128, "int32"), ("ho", 128, "uint16"),
                        ("ge", 128, "bfloat16"), ("rg", 128, "bfloat16"), ("ng", 128, "bfloat16"), ("qn", 64, "bfloat16"),
                        ("qn2", 64, "bfloat16"), ("d", 64, "bfloat16"), ("pp", 128, "bfloat16"), ("mp", 128, "bfloat16"),
-                       ("m", 64, "bfloat16"), ("pm", 64, "bfloat16"), ("qf", 64, "float16"), ("ns", 64, "float16"),
+                       ("m", 64, "bfloat16"), ("pm", 64, "bfloat16"), ("qf", 64, "float16"), ("lm", 128, "float16"), ("ls", 128, "float16"), ("um", 64, "float32"), ("us", 64, "float32"),
                        ("tt", 64, "float16"), ("no", 8, "uint16"), ("nn", 64, "bfloat16"), ("ac", 128, "bfloat16"),
                        ("c0", 64, "bfloat16"), ("c", 64, "bfloat16"), ("ui", 4, "int32"), ("uj", 4, "int32"), ("uw", 4, "float32"),
                        ("uy", 4, "int32"), ("uz", 4, "int32"), ("co", 8, "uint16"), ("df", 64, "bfloat16"), ("yl", 64, "float32")):
@@ -72,15 +73,16 @@ PLACE, SCRATCH = _pack()
 DMAS = 16
 SEMAPHORES = (["sv", "sa", "st", "sg", "ls", "hb0", "hb1", "pr", "bk1", "bk2", "bk3", "bk4", "rc0", "rc1", "rg0", "rg1"]
               + ["rb%d_%d" % (t, h) for t in range(1, VIS) for h in range(2)] + ["dm%d" % i for i in range(DMAS)])
-CYC = 0.00104
-PEC = 0.00052
-HOP = 0.06
+CYC = 0.00083
+PEC = 0.0006
+HOP = 0.12
 MSG = 3.5
-BIAS = 4.0
-PREF = {}
+BIAS = 3.0
+PREF = {"d1": -2, "g0": 1, "z0": 2, "j0": -1, "z1": 4, "r0": 6, "s0": 6, "s1": -2, "i0": -2, "j1": 4, "r1": 2, "c0": 6, "h0": 2,
+        "v0": -2, "g1": -2, "d0": -6, "b1": 1, "v1": 1, "o0": 2}
 GC = 1.56
-VO = (16, 16)
-VB = (16, 16, 16, 16)
+VO = (0, 0)
+VB = (16, 0, 16, 0)
 ORDER = {}
 
 
@@ -265,6 +267,14 @@ def rank_program(g, core, T, topo):
     def arrive(buf, sem, total, after=None, wait=0.0, release=0.0):
         add("X", wait, None, [], [buf], key=sem, amount=total, release=release, extra=() if after is None else (after,))
 
+    def tolist(out, a, tmp, tmp2):
+        n2 = width(a)
+        x, y = W(tmp, 0, n2), W(tmp2, 0, n2)
+        tt(x, a, W("dg", 0, n2), OP.mult)
+        add("V", vcost(n2 * (0.5 if half(x) else 1)),
+            lambda: g.vector.tensor_tensor_scan(ap(y), ap(W("rs", 0, n2)), ap(x), 0.0, OP.mult, OP.add), [x, W("rs", 0, n2)], [y])
+        cp(out, (tmp2, 15, n2, 16))
+
     def R(m, r):
         return (m, 15 - r, 143 - r)
 
@@ -301,7 +311,10 @@ def rank_program(g, core, T, topo):
     tt(W("lt"), W("gt"), W("bo"), OP.mult)
     ts(W("ta"), W("id"), -100.0, OP.mult)
     tt(W("ts"), W("ta"), W("lt"), OP.add)
-    ts(W("wdh"), W("wd"), 1.0, OP.mult)
+    ts(W("jg"), J128, 15, OP.bitwise_and)
+    ts(W("dg"), W("jg"), W("pqf"), OP.is_equal)
+    ts(W("rs"), W("jg"), 0.5, OP.is_gt)
+    ts(W("boh"), W("bo"), 1.0, OP.mult)
     fill(W("par"), 0.0)
     cp(W("par", 0, 1), W("wti"))
     cp(W("par", 1, 2), W("kpi"))
@@ -323,7 +336,6 @@ def rank_program(g, core, T, topo):
     ts(W("tc"), W("lt"), 8.0, OP.mult)
     tt(W("te"), W("tb"), W("tc"), OP.add)
     ts(W("wdf"), W("wd"), 0.5, OP.mult)
-    ts(W("wds"), W("wd"), 1.0 / 16, OP.mult)
     ts(W("ihn"), W("id"), -1.0, OP.mult)
     ts(W("in8"), W("id"), -8.0, OP.mult)
     ts(W("tbc"), W("oh"), -1.0, OP.mult)
@@ -339,7 +351,7 @@ def rank_program(g, core, T, topo):
     tt(W("w8"), W("wa"), W("w7"), OP.add)
     ts(W("b8"), W("bo"), W("w8"), OP.mult, 0.125, OP.mult)
     ts(W("b8x"), W("bo"), W("w8"), OP.mult)
-    ts(W("wdw"), W("wd"), W("par", 0, 1), OP.mult)
+    ts(W("bow"), W("bo"), W("par", 0, 1), OP.mult)
     for k in range(16):
         ts(W("bm", 128 * k, 128 * k + 128), W("bo"), W("oh", k, k + 1), OP.mult, -512.0, OP.mult)
     cp(W("kpb"), W("kpi"))
@@ -411,7 +423,8 @@ def rank_program(g, core, T, topo):
             for k in range(KA, 16):
                 c = 64 * (k - KA)
                 mms(("pd" + s, c, c + 64), [(W("id"), (o, k, 1024, 16)), (W("idn"), W("zz" + s, 0, 64))])
-            act(W(gg, 64 * KA, 1024), ("pd" + s, 0, 64 * (16 - KA)), AF.Relu)
+            if KA < 16:
+                act(W(gg, 64 * KA, 1024), ("pd" + s, 0, 64 * (16 - KA)), AF.Relu)
             for k in range(KA):
                 tt(W(gg, 64 * k, 64 * k + 64), (o, k, 1024, 16), ("pz" + s, 0, 64), OP.is_gt)
             mms(("pn" + s, 0, 64), [(W("ine"), W("em" + s))] + [(R("wd", k), W(gg, 64 * k, 64 * k + 64)) for k in range(16)])
@@ -424,8 +437,8 @@ def rank_program(g, core, T, topo):
                 c = 64 * j
                 ts(W("se" + s, c, c + 64), ("ps" + s, 0, 64), -100.0 + j, OP.is_equal)
                 tt(W("ss" + s, c, c + 64), W("se" + s, c, c + 64), ("ps" + s, 80, 144), OP.mult)
-            mms(("ps" + s, 64, 72), [(R("wdh", r), ("ss" + s, r, 128, 16)) for r in range(16)])
-            cp(W("lo" + s), ("ps" + s, 64, 72))
+            mms(("ps" + s, 144, 272), [(W("boh"), W("ss" + s))])
+            tolist(W("lo" + s), ("ps" + s, 144, 272), "lm" + s, "ls" + s)
             vgather(W(CD + s), W("x"), W("lo" + s), W("zz" + s), OP.min)
             if t == 0:
                 i = send(next1, W("rc" + s), W(CD + s), "rc%d" % h)
@@ -497,13 +510,11 @@ def rank_program(g, core, T, topo):
             ts(W("qf" + s), (PS, 208, 272), MG, OP.add, MG, OP.subtract)
             mms((PS, 144, 208), [(W("id"), W("d" + s)), (W("id"), W("mp" + s, 0, 64)), (W("id"), W("mp" + s, 64, 128))])
             cp(W("pm" + s), (PS, 144, 208))
-            mms((PS, 272, 336), [(W("b8x"), x) for x in parts]
-                + [(W("id8"), W("jb", 64 * h, 64 * h + 64)), (W("in8"), W("qf" + s))])
-            cp(W("ns" + s), (PS, 272, 336))
-            mms(("pn" + s, 192, 196), [(R("wds", r), ("ns" + s, r, 64, 16)) for r in range(16)])
-            cp(W("no" + s, 0, 4), ("pn" + s, 192, 196))
+            nn = [(W("b8x"), W("m" + s)), (W("id8"), W("jb", 64 * h, 64 * h + 64)), (W("in8"), W("qf" + s))]
+            mms((PS, 272, 336), nn)
+            mms((PS, 336, 400), nn + [(W("ihn"), W("sf" + s))])
+            tolist(W("no" + s, 0, 4), (PS, 272, 336), "lm" + s, "ls" + s)
             scatter(W("x"), W("no" + s, 0, 4), W("m" + s))
-            mms((PS, 336, 400), [(W("ih"), W("ns" + s)), (W("ihn"), W("sf" + s))])
             tt(W("tt" + s), W("pm" + s), (PS, 336, 400), OP.mult)
             mms((PS, 80, 144), [(W("ih"), W("sf" + s)), (W("ih"), W("tt" + s))])
         cur[0] = "j"
@@ -524,7 +535,8 @@ def rank_program(g, core, T, topo):
             for k in range(KA, 16):
                 c = 64 * (k - KA)
                 mms(("pd" + s, c, c + 64), [(W("idn"), (o, k, 1024, 16)), (W("id"), W("m" + s))])
-            act(W(gg, 64 * KA, 1024), ("pd" + s, 0, 64 * (16 - KA)), AF.Sign, bias=0.5)
+            if KA < 16:
+                act(W(gg, 64 * KA, 1024), ("pd" + s, 0, 64 * (16 - KA)), AF.Sign, bias=0.5)
             for k in range(KA):
                 tt(W(gg, 64 * k, 64 * k + 64), (o, k, 1024, 16), ("pz" + s, 192, 256), OP.is_le)
             mms(("pn" + s, 0, 64), [(W("ine"), W("em" + s))]
@@ -561,8 +573,8 @@ def rank_program(g, core, T, topo):
         for h in HV:
             s = "_%d" % h
             PS = "ps" + s
-            mms((PS, 64, 68), [(R("wdw", r), ("c" + s, r, 64, 16)) for r in range(16)])
-            cp(W("ui" + s), (PS, 64, 68))
+            mms((PS, 0, 64), [(W("bow"), W("c" + s))])
+            tolist(W("ui" + s), (PS, 0, 64), "um" + s, "us" + s)
             ts(W("uj" + s), W("ui" + s), 4095, OP.bitwise_and)
             ts(W("uw" + s), W("uj" + s), W("k0"), OP.add)
             tt(W("uy" + s), W("uw" + s), W("uj" + s), OP.mult)

@@ -14,10 +14,12 @@ BIG = -8192.0
 SB = {"x": (1024, "bfloat16"), "ce": (EXT, "bfloat16"), "hb": (EXT, "bfloat16"), "sli": (128, "int32"), "zi": (128, "bfloat16"),
       "wti": (1, "int32"), "kpi": (1, "int32"), "par": (8, "bfloat16"), "pr": (32, "bfloat16"),
       "pi": (1, "int32"), "pg": (1, "int32"), "pq": (1, "int32"), "ji": (144, "int32"), "jg": (128, "int32"),
-      "pf": (1, "float32"), "pgf": (1, "float32"), "pqf": (1, "float32"), "pwf": (1, "float32"), "oh": (16, "float32"),
+      "pf": (1, "float32"), "pgf": (1, "float32"), "pqf": (1, "float32"), "pwf": (1, "float32"), "oh": (16, "float32"), "ohs": (16, "float32"),
       "w7": (1, "int32"), "wa": (1, "float32"), "w8": (1, "float32"), "cc": (1, "float32"), "ccb": (1, "float32"),
       "bo": (128, "bfloat16"), "bo100": (128, "bfloat16"), "id": (128, "bfloat16"), "idn": (128, "bfloat16"), "id2": (128, "bfloat16"),
-      "id8": (128, "bfloat16"), "idh": (128, "bfloat16"), "ine": (128, "bfloat16"), "gt": (128, "bfloat16"), "lt": (128, "bfloat16"),
+      "id8": (128, "bfloat16"), "id50": (128, "bfloat16"), "bo50": (128, "bfloat16"),
+      "bo05": (128, "bfloat16"), "ul": (256, "int32"), "um2": (256, "int32"), "uw2": (256, "float32"), "uy2": (256, "int32"),
+      "uh": (256, "int32"), "j1k": (1024, "bfloat16"), "rs1k": (1024, "bfloat16"), "ine": (128, "bfloat16"), "gt": (128, "bfloat16"), "lt": (128, "bfloat16"),
       "ta": (128, "bfloat16"), "ts": (128, "bfloat16"), "tb": (128, "bfloat16"), "te": (128, "bfloat16"), "tc": (128, "bfloat16"),
       "wd": (144, "bfloat16"), "wdf": (144, "bfloat16"), "bow": (128, "bfloat16"), "boh": (128, "float16"), "dg": (128, "bfloat16"),
       "rs": (128, "bfloat16"),
@@ -28,6 +30,8 @@ SB = {"x": (1024, "bfloat16"), "ce": (EXT, "bfloat16"), "hb": (EXT, "bfloat16"),
 for _t in range(VIS):
     SB["wq%d" % _t] = (128, "bfloat16")
     SB["kc%d" % _t] = (1, "float32")
+    SB["ct%d" % _t] = (NB, "bfloat16")
+    SB["uo%d" % _t] = (256, "uint16")
     if _t:
         SB["bk%d" % _t] = (NB, "bfloat16")
 for _h in range(2):
@@ -39,9 +43,10 @@ for _h in range(2):
                        ("ge", 128, "bfloat16"), ("rg", 128, "bfloat16"), ("ng", 128, "bfloat16"), ("qn", 64, "bfloat16"),
                        ("qn2", 64, "bfloat16"), ("d", 64, "bfloat16"), ("pp", 128, "bfloat16"), ("mp", 128, "bfloat16"),
                        ("m", 64, "bfloat16"), ("pm", 64, "bfloat16"), ("qf", 64, "float16"), ("lm", 128, "float16"), ("ls", 128, "float16"), ("um", 64, "float32"), ("us", 64, "float32"),
-                       ("tt", 64, "float16"), ("no", 8, "uint16"), ("nn", 64, "bfloat16"), ("ac", 128, "bfloat16"),
-                       ("c0", 64, "bfloat16"), ("c", 64, "bfloat16"), ("ui", 4, "int32"), ("uj", 4, "int32"), ("uw", 4, "float32"),
-                       ("uy", 4, "int32"), ("uz", 4, "int32"), ("co", 8, "uint16"), ("df", 64, "bfloat16"), ("yl", 64, "float32")):
+                       ("tt", 64, "float16"), ("no", 8, "uint16"), ("nn", 64, "bfloat16"), ("mo", 1024, "bfloat16"),
+                       ("ms", 1024, "bfloat16"), ("c", 64, "bfloat16"), ("ui", 64, "int32"), ("uj", 64, "int32"),
+                       ("uw", 64, "float32"), ("uy", 64, "int32"), ("uz", 64, "int32"),
+                       ("co", 8, "uint16"), ("df", 64, "bfloat16"), ("yl", 64, "float32")):
         SB["%s_%d" % (_n, _h)] = (_w, _d)
     for _t in range(1, VIS):
         SB["bs%d_%d" % (_t, _h)] = (64, "bfloat16")
@@ -71,18 +76,20 @@ def _pack():
 
 PLACE, SCRATCH = _pack()
 DMAS = 16
-SEMAPHORES = (["sv", "sa", "st", "sg", "ls", "hb0", "hb1", "pr", "bk1", "bk2", "bk3", "bk4", "rc0", "rc1", "rg0", "rg1"]
+SEMAPHORES = (["sv", "sa", "st", "sg", "ls", "hb0", "pr", "bk1", "bk2", "bk3", "bk4", "rc0", "rc1", "rg0", "rg1"]
               + ["rb%d_%d" % (t, h) for t in range(1, VIS) for h in range(2)] + ["dm%d" % i for i in range(DMAS)])
 CYC = 0.00083
 PEC = 0.0006
-HOP = 0.12
+HOP = 0.17
 MSG = 3.5
 BIAS = 3.0
-PREF = {"d1": -2, "g0": 1, "z0": 2, "j0": -1, "z1": 4, "r0": 6, "s0": 6, "s1": -2, "i0": -2, "j1": 4, "r1": 2, "c0": 6, "h0": 2,
-        "v0": -2, "g1": -2, "d0": -6, "b1": 1, "v1": 1, "o0": 2}
+PREF = {"t1": -30, "n0": 2, "n1": 1, "g0": -4, "o0": 1, "h0": 4, "j0": 2, "z1": -2, "h1": 1, "b0": 1, "r1": -6, "s0": -6, "j1": 4,
+        "o1": -6, "s1": 1, "r0": -2, "d0": 4, "v1": -1, "g1": -6, "i0": 6, "i1": -4, "c1": -2}
 GC = 1.56
+CT = (1, 1, 1, 1, 1)
+KR = 8
 VO = (0, 0)
-VB = (16, 0, 16, 0)
+VB = (16, 24, 24, 0)
 ORDER = {}
 
 
@@ -90,10 +97,11 @@ def helpers(T, topo, r):
     n = len(T.cores)
     own = T.cores[r]
     out = []
-    for same, ts in ((True, (1, 3)), (False, (2, 4))):
+    for i, same in enumerate((True, False)):
         for c in topo.cores_of(own):
-            if c != own and (topo.die(c) == topo.die(own)) == same and all(topo.may_write(c, T.cores[(r - 1 - t) % n]) for t in ts):
-                out.append((c, ts))
+            if c != own and (topo.die(c) == topo.die(own)) == same \
+                    and all(topo.may_write(c, T.cores[(r - 1 - t) % n]) for t in range(1, VIS)):
+                out.append((c, i))
                 break
     return out
 
@@ -102,18 +110,17 @@ def pieces(t):
     return ((97 * t, CUT), (CUT, 97 * t + NB))
 
 
-def forward(g, core, T, topo, r, ts):
+def forward(g, core, T, topo, r, i):
     n = len(T.cores)
     hb, sent = T[PLACE["hb"][0]], 0
-    for t in ts:
+    g.wait_ge(T.sem.hb0, len(onchip(T, topo, r, core)))
+    for t in range(1, VIS):
         dst = T.cores[(r - 1 - t) % n]
         rid, pid = topo.addr(dst, core)
-        for i, (a, b) in enumerate(pieces(t)):
-            if t == ts[0]:
-                g.wait_ge(T.sem["hb%d" % i], len(onchip(T, topo, r, core)))
-            g.remote_dma(out_ap=T["s_bk%d" % t][:, a - 97 * t:b - 97 * t], in_ap=hb[:, a:b], remote_sem=T.sem["bk%d" % t],
-                         local_sem=T.sem.ls, pid=pid, routing_id=rid, dma_engine_mask=topo.mask(core, dst))
-            sent += len(topo.engines(core, dst))
+        a, b = pieces(t)[i]
+        g.remote_dma(out_ap=T["s_bk%d" % t][:, a - 97 * t:b - 97 * t], in_ap=hb[:, a:b], remote_sem=T.sem["bk%d" % t],
+                     local_sem=T.sem.ls, pid=pid, routing_id=rid, dma_engine_mask=topo.mask(core, dst))
+        sent += len(topo.engines(core, dst))
     g.wait_ge(T.sem.ls, sent)
 
 
@@ -129,9 +136,9 @@ def rank_program(g, core, T, topo):
     rank = T.rank_of(core)
     if rank is None:
         for r in range(n):
-            for c, ts in helpers(T, topo, r):
+            for c, i in helpers(T, topo, r):
                 if c == core:
-                    forward(g, core, T, topo, r, ts)
+                    forward(g, core, T, topo, r, i)
         return
     ops = []
     hist, banks = {}, {}
@@ -156,7 +163,7 @@ def rank_program(g, core, T, topo):
 
     def add(q, cost, fn, r=(), w=(), key=None, amount=1, release=0.0, extra=()):
         i = len(ops)
-        deps = set(extra)
+        deps = set()
         for items, wr in ((r, False), (w, True)):
             for x in items:
                 if psum(x):
@@ -168,17 +175,19 @@ def rank_program(g, core, T, topo):
                         deps.update(e[1][1][-1:])
                     e[1][1].append(i)
                 elif x[0] in SB:
-                    for (a, e, j, jw) in hist.setdefault(x[0], []):
-                        if a < x[2] and x[1] < e and (wr or jw):
+                    st = x[3] if len(x) > 3 else 1
+                    for (a, e, j, jw, s2) in hist.setdefault(x[0], []):
+                        if a < x[2] and x[1] < e and (wr or jw) and (st == 1 or s2 != st or (a - x[1]) % st == 0):
                             deps.add(j)
         for x in r:
             if x[0] in SB:
-                hist[x[0]].append((x[1], x[2], i, False))
+                hist[x[0]].append((x[1], x[2], i, False, x[3] if len(x) > 3 else 1))
         for x in w:
             if x[0] in SB:
-                hist[x[0]] = [y for y in hist[x[0]] if not (x[1] <= y[0] and y[1] <= x[2])] + [(x[1], x[2], i, True)]
+                st = x[3] if len(x) > 3 else 1
+                hist[x[0]] = [y for y in hist[x[0]] if st > 1 or not (x[1] <= y[0] and y[1] <= x[2])] + [(x[1], x[2], i, True, st)]
         deps.discard(i)
-        ops.append([q, KEY.get(q) if key is None else key, amount, fn, cost, sorted(deps), release, bias(r, w)])
+        ops.append([q, KEY.get(q) if key is None else key, amount, fn, cost, sorted(deps | set(extra)), release, bias(r, w), sorted(deps)])
         return i
 
     def bias(r, w):
@@ -219,8 +228,11 @@ def rank_program(g, core, T, topo):
         return add("V", vcost(width(out) * 0.5), lambda: g.vector.memset(ap(out), v), [], [out])
 
     def act(out, a, func, bias=0.0, scale=1.0):
-        rd = [a] + ([bias] if isap(bias) else [])
-        return add("A", vcost(width(out)), lambda: g.scalar.activation(ap(out), ap(a), func, bias=val(bias), scale=scale), rd, [out])
+        rd = [a] + [x for x in (bias, scale) if isap(x)]
+        return add("A", vcost(width(out)), lambda: g.scalar.activation(ap(out), ap(a), func, bias=val(bias), scale=val(scale)), rd, [out])
+
+    def times(out, a, s):
+        return act(out, a, AF.Identity, scale=s)
 
     def agather(out, win, off, share):
         for q, a, b in (("V", 64 - share, 64), ("A", 0, 64 - share)):
@@ -267,13 +279,16 @@ def rank_program(g, core, T, topo):
     def arrive(buf, sem, total, after=None, wait=0.0, release=0.0):
         add("X", wait, None, [], [buf], key=sem, amount=total, release=release, extra=() if after is None else (after,))
 
-    def tolist(out, a, tmp, tmp2):
+    def tolist(out, a, tmp, tmp2, plus=None):
         n2 = width(a)
         x, y = W(tmp, 0, n2), W(tmp2, 0, n2)
         tt(x, a, W("dg", 0, n2), OP.mult)
         add("V", vcost(n2 * (0.5 if half(x) else 1)),
             lambda: g.vector.tensor_tensor_scan(ap(y), ap(W("rs", 0, n2)), ap(x), 0.0, OP.mult, OP.add), [x, W("rs", 0, n2)], [y])
-        cp(out, (tmp2, 15, n2, 16))
+        if plus:
+            ts(out, (tmp2, 15, n2, 16), plus, OP.add)
+        else:
+            cp(out, (tmp2, 15, n2, 16))
 
     def R(m, r):
         return (m, 15 - r, 143 - r)
@@ -302,11 +317,11 @@ def rank_program(g, core, T, topo):
     ts(W("pwf"), W("pg"), 16.0, OP.mult, 15.0, OP.add)
     ts(W("id"), J128, W("pf"), OP.is_equal)
     ts(W("ih"), W("id"), 1.0, OP.mult)
-    ts(W("idn"), W("id"), -1.0, OP.mult)
+    times(W("idn"), W("id"), -1.0)
     ts(W("bo"), W("jg"), W("pgf"), OP.is_equal)
     ts(W("wd"), W("ji"), W("pwf"), OP.is_equal)
     ts(W("oh"), W("ji", 0, 16), W("pqf"), OP.is_equal)
-    ts(W("ine"), W("id"), BIG, OP.mult)
+    times(W("ine"), W("id"), BIG)
     ts(W("gt"), J128, W("pf"), OP.is_gt)
     tt(W("lt"), W("gt"), W("bo"), OP.mult)
     ts(W("ta"), W("id"), -100.0, OP.mult)
@@ -328,14 +343,16 @@ def rank_program(g, core, T, topo):
         ts(W("wq%d" % t), W("bo"), (src, c, c + 1), OP.mult, 2.0 ** -12, OP.mult)
         ts(W("kc%d" % t), (src, c + 1, c + 2), 2.0 ** 17, OP.mult)
     weights(0, "par", 0)
-    ts(W("id2"), W("id"), 2.0, OP.mult)
-    ts(W("id8"), W("id"), 8.0, OP.mult)
-    ts(W("idh"), W("id"), -100.0, OP.mult)
-    ts(W("bo100"), W("bo"), 100.0, OP.mult)
-    ts(W("tb"), W("id"), -8.0, OP.mult)
-    ts(W("tc"), W("lt"), 8.0, OP.mult)
+    times(W("id2"), W("id"), 2.0)
+    times(W("id8"), W("id"), 8.0)
+    times(W("id50"), W("id"), 50.0)
+    times(W("bo50"), W("bo"), -50.0)
+    times(W("bo05"), W("bo"), -0.5)
+    times(W("bo100"), W("bo"), 100.0)
+    times(W("tb"), W("id"), -8.0)
+    times(W("tc"), W("lt"), 8.0)
     tt(W("te"), W("tb"), W("tc"), OP.add)
-    ts(W("wdf"), W("wd"), 0.5, OP.mult)
+    times(W("wdf"), W("wd"), 0.5)
     ts(W("ihn"), W("id"), -1.0, OP.mult)
     ts(W("in8"), W("id"), -8.0, OP.mult)
     ts(W("tbc"), W("oh"), -1.0, OP.mult)
@@ -352,11 +369,34 @@ def rank_program(g, core, T, topo):
     ts(W("b8"), W("bo"), W("w8"), OP.mult, 0.125, OP.mult)
     ts(W("b8x"), W("bo"), W("w8"), OP.mult)
     ts(W("bow"), W("bo"), W("par", 0, 1), OP.mult)
+    ts(W("ohs"), W("oh"), -512.0, OP.mult)
     for k in range(16):
-        ts(W("bm", 128 * k, 128 * k + 128), W("bo"), W("oh", k, k + 1), OP.mult, -512.0, OP.mult)
+        times(W("bm", 128 * k, 128 * k + 128), W("bo"), W("ohs", k, k + 1))
     cp(W("kpb"), W("kpi"))
     mms(("ps_0", 72, 73), [(W("bm", 0, 128), W("kpb"))])
     ts(W("k0"), ("ps_0", 72, 73), -32.0 / 512, OP.mult)
+    cur[0] = "t"
+    add("G", 0.6, lambda: g.iota(ap(W("ul")), [[16, 256]], 0, 0), [], [W("ul")])
+    add("G", 2.0, lambda: g.iota(ap(W("j1k")), [[0, 64], [1, 16]], 0, 0, allow_small_or_imprecise_dtypes=True), [], [W("j1k")])
+    ts(W("rs1k"), W("j1k"), 0.5, OP.is_gt)
+    ts(W("um2"), W("ul"), W("pqf"), OP.add)
+    ts(W("uw2"), W("um2"), W("k0"), OP.add)
+    tt(W("uy2"), W("uw2"), W("um2"), OP.mult)
+    ts(W("uh"), W("uy2"), 5, OP.arith_shift_right, 4095, OP.bitwise_and)
+    for t in range(VIS):
+        ts(W("uo%d" % t), W("uh"), 97.0 * t, OP.add)
+    cur[0] = "-"
+
+    def own_book(t, after):
+        if not CT[t]:
+            return
+        k = cur[0]
+        cur[0] = "t"
+        for c in range(8):
+            out, win, off = W("ct%d" % t, 512 * c, 512 * c + 512), W("ce"), W("uo%d" % t, 32 * c, 32 * c + 32)
+            add("A", 0.065 + GC * CYC * 512, lambda out=out, win=win, off=off:
+                g.scalar.activation(ap(out), ap(win).indirect(ap(off)), AF.Copy), [win, off], [out], extra=[after])
+        cur[0] = k
 
     def params(after):
         add("G", 2.0, fused, [W("par")], [], key="", extra=[after])
@@ -375,16 +415,17 @@ def rank_program(g, core, T, topo):
     arrive(W("pr"), "pr", nsm * (VIS - 1), release=12.0)
 
     def book(i, a, b, after):
+        c = helpers(T, topo, rank)[i][0]
+        rid, pid = topo.addr(c, core)
+        e = onchip(T, topo, rank, c)
+
         def fn():
-            for c, _ts in helpers(T, topo, rank):
-                rid, pid = topo.addr(c, core)
-                e = onchip(T, topo, rank, c)
-                g.remote_dma(out_ap=ap(W("hb", a, b)), in_ap=ap(W("ce", a, b)), remote_sem=T.sem["hb%d" % i], local_sem=T.sem.ls,
-                             pid=pid, routing_id=rid, dma_engine_mask=sum(1 << x for x in e))
-        add("G", 2.0, fn, [W("ce", a, b)], [], key="", extra=[after])
-        local[0] += sum(len(onchip(T, topo, rank, c)) for c, _ts in helpers(T, topo, rank))
+            g.remote_dma(out_ap=ap(W("hb", a, b)), in_ap=ap(W("ce", a, b)), remote_sem=T.sem.hb0, local_sem=T.sem.ls,
+                         pid=pid, routing_id=rid, dma_engine_mask=sum(1 << x for x in e))
+        add("G", 1.0, fn, [W("ce", a, b)], [], key="", extra=[after])
+        local[0] += len(e)
     for t in range(1, VIS):
-        arrive(W("bk%d" % t), "bk%d" % t, 2 * nsm, release=(0, 22.0, 24.0, 32.0, 34.0)[t])
+        arrive(W("bk%d" % t), "bk%d" % t, 2 * nsm, release=(0, 24.0, 32.0, 40.0, 48.0)[t])
 
     HV = range(2)
     for h in HV:
@@ -399,7 +440,7 @@ def rank_program(g, core, T, topo):
     def slots_in(s, first):
         SP = ("ps" + s, 80, 144)
         cp(W("so" + s), SP)
-        ts(W("em" + s), SP, -0.5, OP.is_lt)
+        act(W("em" + s), SP, AF.Relu, scale=-1.0)
         if not first:
             cp(W("sf" + s), SP)
 
@@ -447,6 +488,7 @@ def rank_program(g, core, T, topo):
             book(0, 0, CUT, i)
             book(1, CUT, EXT, i)
             params(i)
+            own_book(0, i)
         cur[0] = "h"
         for h in HV:
             s = "_%d" % h
@@ -469,11 +511,14 @@ def rank_program(g, core, T, topo):
             for j in range(2):
                 c = 64 * j
                 agather(W("b" + s, 1024 * j, 1024 * j + 1024), win, W("ho" + s, c, c + 64), VB[2 * h + j])
+                last = len(ops) - 1
                 for m in range(16):
                     e = 1024 * j + 64 * m
                     tt(W("gb" + s, e, e + 64), ("b" + s, 1024 * j + m, 1024 * j + 1024, 16), ("pz" + s, 64 + c, 128 + c), OP.is_le)
                 mms(("pn" + s, 64 + c, 128 + c), [(R("wd", m), W("gb" + s, 1024 * j + 64 * m, 1024 * j + 64 * m + 64)) for m in range(16)])
                 ts(W(GE + s, c, c + 64), ("pn" + s, 64 + c, 128 + c), 8.5, OP.is_ge)
+            if t < VIS - 1 and h == 1:
+                own_book(t + 1, last)
             if t == 0:
                 i = send(prev1, W("rg" + s), W(GE + s), "rg%d" % h)
                 arrive(W("rg" + s), "rg%d" % h, nsm, after=i, wait=MSG)
@@ -491,10 +536,9 @@ def rank_program(g, core, T, topo):
             mms((PS, 0, 64), [(W("bo100"), W(se, 0, 64)), (W("bo"), W(ge, 0, 64))] + bits)
             ts(W(ng, 0, 64), (PS, 0, 64), thr, OP.is_ge)
             mms((PS, 400, 464), [(W("bo"), W("cb")), (W("on32"), W(ng, 0, 64))])
-            ts(W("qn" + s), (PS, 400, 464), MG, OP.add, MG, OP.subtract)
-            mms((PS, 0, 64), [(W("bo100"), W(se, 64, 128)), (W("bo"), W(ge, 64, 128)), (W("idh"), W(ng, 0, 64)), (W("on16"), W(ng, 0, 64)),
-                              (W("id2"), W("qn" + s))])
-            ts(W(ng, 64, 128), (PS, 0, 64), thr, OP.is_ge)
+            mms((PS, 0, 64), [(W("bo50"), W(se, 64, 128)), (W("bo05"), W(ge, 64, 128)), (W("id50"), W(ng, 0, 64)), (W("on32"), W(ng, 0, 64))])
+            ts(W("qn" + s), (PS, 400, 464), MG, OP.add, MG + (100 + AT[t]) // 2, OP.subtract)
+            tt(W(ng, 64, 128), W("qn" + s), (PS, 0, 64), OP.is_gt if AT[t] % 2 else OP.is_ge)
             for j in range(2):
                 c = 64 * j
                 tt(W("pp" + s, c, c + 64), W(ng, c, c + 64), (PS, 144 + c, 208 + c), OP.mult)
@@ -560,30 +604,35 @@ def rank_program(g, core, T, topo):
                 p = ("pd" if k < 8 else "pn") + s
                 c = 64 * (k % 8)
                 mms((p, c, c + 64), [(W("id"), (o, k, 1024, 16)), (W("bm", 128 * k, 128 * k + 128), W("nn" + s))])
-            for k in range(0, 16, 2):
-                p = ("pd" if k < 8 else "pn") + s
-                c = 64 * (k % 8)
-                if k == 0:
-                    ts(W("ac" + s), (p, c, c + 128), 0.0, OP.max)
+            for k in range(16):
+                p = (("pd" if k < 8 else "pn") + s, 64 * (k % 8), 64 * (k % 8) + 64)
+                if k < KR:
+                    act(("mo" + s, k, 1024, 16), p, AF.Relu)
                 else:
-                    tt(W("ac" + s), W("ac" + s), (p, c, c + 128), OP.max)
-            tt(W("c0" + s), W("ac" + s, 0, 64), ("pz" + s, 192, 256), OP.max)
-            tt(W("c" + s), W("ac" + s, 64, 128), W("c0" + s), OP.max)
+                    ts(("mo" + s, k, 1024, 16), p, 0.0, OP.max)
+            add("V", vcost(512), lambda s=s: g.vector.tensor_tensor_scan(ap(W("ms" + s)), ap(W("rs1k")), ap(W("mo" + s)), 0.0,
+                                                                        OP.mult, OP.max), [W("rs1k"), W("mo" + s)], [W("ms" + s)])
+            tt(W("c" + s), ("ms" + s, 15, 1024, 16), ("pz" + s, 192, 256), OP.max)
         cur[0] = "z"
         for h in HV:
             s = "_%d" % h
             PS = "ps" + s
             mms((PS, 0, 64), [(W("bow"), W("c" + s))])
-            tolist(W("ui" + s), (PS, 0, 64), "um" + s, "us" + s)
+            cp(W("ui" + s), (PS, 0, 64))
             ts(W("uj" + s), W("ui" + s), 4095, OP.bitwise_and)
-            ts(W("uw" + s), W("uj" + s), W("k0"), OP.add)
-            tt(W("uy" + s), W("uw" + s), W("uj" + s), OP.mult)
-            ts(W("uz" + s), W("uy" + s), 5, OP.arith_shift_right, 4095, OP.bitwise_and)
-            ts(W("co" + s, 0, 4), W("uz" + s), 97.0 * t, OP.add)
-            vgather(W("df" + s), W("ce"), W("co" + s, 0, 4), W("c" + s), OP.subtract)
+            if CT[t]:
+                tolist(W("co" + s, 0, 4), W("uj" + s), "um" + s, "us" + s)
+                vgather(W("df" + s), W("ct%d" % t), W("co" + s, 0, 4), W("c" + s), OP.subtract)
+            else:
+                ts(W("uw" + s), W("uj" + s), W("k0"), OP.add)
+                tt(W("uy" + s), W("uw" + s), W("uj" + s), OP.mult)
+                ts(W("uz" + s), W("uy" + s), 5, OP.arith_shift_right, 4095, OP.bitwise_and)
+                tolist(W("co" + s, 0, 4), W("uz" + s), "um" + s, "us" + s, 97.0 * t)
+                vgather(W("df" + s), W("ce"), W("co" + s, 0, 4), W("c" + s), OP.subtract)
+            if t < VIS - 1:
+                act(("pz" + s, 0, 64), W("df" + s), AF.Abs)
             act(W("zz" + s, 0, 64), W("df" + s), AF.Abs)
             if t < VIS - 1:
-                mms(("pz" + s, 0, 64), [(W("id"), W("zz" + s, 0, 64))])
                 act(W("zz" + s, 64, 128), W("df" + s), AF.Abs)
             else:
                 dma(("yz", 64 * h, 64 * h + 64), W("zz" + s, 0, 64))
@@ -593,7 +642,7 @@ def rank_program(g, core, T, topo):
     known = {q: {} for q in QUEUE}
     count, clock = {}, {}
     for i in ORDER["order"]:
-        q, key, amount, fn, _c, deps, _r, _b = ops[i]
+        q, key, amount, fn, _c, _e, _r, _b, deps = ops[i]
         if q == "X":
             clock[i] = {key: amount}
             count[key] = amount

from concourse.bass import DstId, RemoteDMATransfer
from concourse.mybir import dt, AluOpType, AxisListType, ActivationFunctionType

OP = AluOpType
AF = ActivationFunctionType
VIS, NB = 5, 4096
AT = [5, 4, 4, 3, 3]
EXT = 4496
CUT = 2304
MG = 12582912.0
KA = 16
BIG = -8192.0

SB = {"x": (1024, "bfloat16"), "ce": (EXT, "bfloat16"), "hb": (EXT, "bfloat16"), "sli": (128, "int32"), "zi": (128, "bfloat16"),
      "wti": (1, "int32"), "kpi": (1, "int32"), "par": (8, "bfloat16"), "pr": (32, "bfloat16"),
      "pi": (1, "int32"), "pg": (1, "int32"), "pq": (1, "int32"), "ji": (144, "int32"), "jg": (128, "int32"),
      "pf": (1, "float32"), "pgf": (1, "float32"), "pqf": (1, "float32"), "pwf": (1, "float32"), "oh": (16, "float32"), "ohs": (16, "float32"),
      "w7": (1, "int32"), "wa": (1, "float32"), "w8": (1, "float32"), "cc": (1, "float32"), "ccb": (1, "float32"),
      "bo": (128, "bfloat16"), "bo100": (128, "bfloat16"), "id": (128, "bfloat16"), "idn": (128, "bfloat16"), "id2": (128, "bfloat16"),
      "id8": (128, "bfloat16"), "id50": (128, "bfloat16"), "bo50": (128, "bfloat16"),
      "bo05": (128, "bfloat16"), "ul": (256, "int32"), "um2": (256, "int32"), "uw2": (256, "float32"), "uy2": (256, "int32"),
      "uh": (256, "int32"), "j1k": (1024, "bfloat16"), "rs1k": (1024, "bfloat16"), "ine": (128, "bfloat16"), "gt": (128, "bfloat16"), "lt": (128, "bfloat16"),
      "ta": (128, "bfloat16"), "ts": (128, "bfloat16"), "tb": (128, "bfloat16"), "te": (128, "bfloat16"), "tc": (128, "bfloat16"),
      "wd": (144, "bfloat16"), "wdf": (144, "bfloat16"), "bow": (128, "bfloat16"), "boh": (128, "float16"), "dg": (128, "bfloat16"),
      "rs": (128, "bfloat16"),
      "ih": (128, "float16"), "ihn": (128, "float16"), "in8": (128, "float16"), "bm": (2048, "bfloat16"), "one": (128, "bfloat16"),
      "ca": (128, "bfloat16"), "cb": (64, "bfloat16"), "cq": (64, "bfloat16"), "on32": (128, "bfloat16"), "on16": (128, "bfloat16"),
      "jb": (128, "bfloat16"), "b8": (128, "bfloat16"), "b8x": (128, "bfloat16"), "thr": (1, "float32"), "tbc": (16, "float32"),
      "k0": (1, "float32"), "kpb": (1, "bfloat16")}
for _t in range(VIS):
    SB["wq%d" % _t] = (128, "bfloat16")
    SB["kc%d" % _t] = (1, "float32")
    SB["ct%d" % _t] = (NB, "bfloat16")
    SB["uo%d" % _t] = (256, "uint16")
    if _t:
        SB["bk%d" % _t] = (NB, "bfloat16")
for _h in range(2):
    for _n, _w, _d in (("o0", 1024, "bfloat16"), ("o1", 1024, "bfloat16"), ("b", 2048, "bfloat16"), ("gg", 1024, "bfloat16"),
                       ("gb", 2048, "bfloat16"), ("zz", 128, "bfloat16"), ("so", 64, "uint16"), ("sf", 64, "float16"),
                       ("em", 64, "bfloat16"), ("op", 64, "bfloat16"), ("se", 128, "bfloat16"), ("ss", 128, "float16"),
                       ("lo", 8, "uint16"), ("cd", 128, "bfloat16"), ("ci", 128, "bfloat16"), ("gi", 128, "bfloat16"), ("rc", 128, "bfloat16"), ("qb", 128, "bfloat16"),
                       ("ww", 128, "float32"), ("y", 128, "int32"), ("y2", 128, "int32"), ("ho", 128, "uint16"),
                       ("ge", 128, "bfloat16"), ("rg", 128, "bfloat16"), ("ng", 128, "bfloat16"), ("qn", 64, "bfloat16"),
                       ("qn2", 64, "bfloat16"), ("d", 64, "bfloat16"), ("pp", 128, "bfloat16"), ("mp", 128, "bfloat16"),
                       ("m", 64, "bfloat16"), ("pm", 64, "bfloat16"), ("qf", 64, "float16"), ("lm", 128, "float16"), ("ls", 128, "float16"), ("um", 64, "float32"), ("us", 64, "float32"),
                       ("tt", 64, "float16"), ("no", 8, "uint16"), ("nn", 64, "bfloat16"), ("mo", 1024, "bfloat16"),
                       ("ms", 1024, "bfloat16"), ("c", 64, "bfloat16"), ("ui", 64, "int32"), ("uj", 64, "int32"),
                       ("uw", 64, "float32"), ("uy", 64, "int32"), ("uz", 64, "int32"),
                       ("co", 8, "uint16"), ("df", 64, "bfloat16"), ("yl", 64, "float32")):
        SB["%s_%d" % (_n, _h)] = (_w, _d)
    for _t in range(1, VIS):
        SB["bs%d_%d" % (_t, _h)] = (64, "bfloat16")
        SB["rb%d_%d" % (_t, _h)] = (64, "bfloat16")


def _pack():
    place, scratch, fill = {}, {}, {}
    for n in sorted(SB):
        w, d = SB[n]
        if w >= 1024:
            scratch["s_" + n] = ("sbuf", [128, w], d)
            place[n] = ("s_" + n, 0, d)
        else:
            step = (w + 15) // 16 * 16
            place[n] = ("k_" + d, fill.setdefault(d, 0), d)
            fill[d] += step
    for d in fill:
        scratch["k_" + d] = ("sbuf", [128, fill[d]], d)
    for h in range(2):
        for p in ("pz", "pn", "ps", "pd"):
            n = "%s_%d" % (p, h)
            scratch[n] = ("psum", [128, 512], "float32")
            place[n] = (n, 0, "float32")
    return place, scratch


PLACE, SCRATCH = _pack()
DMAS = 16
SEMAPHORES = (["sv", "sa", "st", "sg", "ls", "hb0", "pr", "bk1", "bk2", "bk3", "bk4", "rc0", "rc1", "rg0", "rg1"]
              + ["rb%d_%d" % (t, h) for t in range(1, VIS) for h in range(2)] + ["dm%d" % i for i in range(DMAS)])
CYC = 0.00083
PEC = 0.0006
HOP = 0.17
MSG = 3.5
BIAS = 3.0
PREF = {"t1": -30, "n0": 2, "n1": 1, "g0": -4, "o0": 1, "h0": 4, "j0": 2, "z1": -2, "h1": 1, "b0": 1, "r1": -6, "s0": -6, "j1": 4,
        "o1": -6, "s1": 1, "r0": -2, "d0": 4, "v1": -1, "g1": -6, "i0": 6, "i1": -4, "c1": -2}
GC = 1.56
CT = (1, 1, 1, 1, 1)
KR = 8
VO = (0, 0)
VB = (16, 24, 24, 0)
ORDER = {}


def helpers(T, topo, r):
    n = len(T.cores)
    own = T.cores[r]
    out = []
    for i, same in enumerate((True, False)):
        for c in topo.cores_of(own):
            if c != own and (topo.die(c) == topo.die(own)) == same \
                    and all(topo.may_write(c, T.cores[(r - 1 - t) % n]) for t in range(1, VIS)):
                out.append((c, i))
                break
    return out


def pieces(t):
    return ((97 * t, CUT), (CUT, 97 * t + NB))


def forward(g, core, T, topo, r, i):
    n = len(T.cores)
    hb, sent = T[PLACE["hb"][0]], 0
    g.wait_ge(T.sem.hb0, len(onchip(T, topo, r, core)))
    for t in range(1, VIS):
        dst = T.cores[(r - 1 - t) % n]
        rid, pid = topo.addr(dst, core)
        a, b = pieces(t)[i]
        g.remote_dma(out_ap=T["s_bk%d" % t][:, a - 97 * t:b - 97 * t], in_ap=hb[:, a:b], remote_sem=T.sem["bk%d" % t],
                     local_sem=T.sem.ls, pid=pid, routing_id=rid, dma_engine_mask=topo.mask(core, dst))
        sent += len(topo.engines(core, dst))
    g.wait_ge(T.sem.ls, sent)


def onchip(T, topo, r, helper):
    n = len(T.cores)
    own = T.cores[r]
    off = topo.engines(own, T.cores[(r + 1) % n])
    return [e for e in topo.engines(own, helper) if e not in off]


def rank_program(g, core, T, topo):
    n = len(T.cores)
    rank = T.rank_of(core)
    if rank is None:
        for r in range(n):
            for c, i in helpers(T, topo, r):
                if c == core:
                    forward(g, core, T, topo, r, i)
        return
    ops = []
    hist, banks = {}, {}
    ndma, local, cur = [0], [0], ["-"]
    QUEUE = {"V": g.vector, "A": g.scalar, "T": g.tensor, "G": g, "S": g.sync}
    KEY = {"V": "sv", "A": "sa", "T": "st", "G": "sg"}

    def ap(x):
        name, a, b = x[0], x[1], x[2]
        if name in PLACE:
            buf, off, _d = PLACE[name]
            if len(x) > 3:
                return T[buf][:, off + a:off + b:x[3]]
            return T[buf][:, off + a:off + b]
        return T[name][:, a:b]

    def W(name, a=0, b=None):
        return (name, a, SB[name][0] if b is None else b)

    def psum(x):
        return x[0] not in SB and x[0] in PLACE

    def add(q, cost, fn, r=(), w=(), key=None, amount=1, release=0.0, extra=()):
        i = len(ops)
        deps = set()
        for items, wr in ((r, False), (w, True)):
            for x in items:
                if psum(x):
                    e = banks.setdefault(x[0], [(None, []), (None, [])])
                    if e[1][0] != q:
                        e[0], e[1] = e[1], (q, [])
                    deps.update(e[0][1])
                    if q == "T":
                        deps.update(e[1][1][-1:])
                    e[1][1].append(i)
                elif x[0] in SB:
                    st = x[3] if len(x) > 3 else 1
                    for (a, e, j, jw, s2) in hist.setdefault(x[0], []):
                        if a < x[2] and x[1] < e and (wr or jw) and (st == 1 or s2 != st or (a - x[1]) % st == 0):
                            deps.add(j)
        for x in r:
            if x[0] in SB:
                hist[x[0]].append((x[1], x[2], i, False, x[3] if len(x) > 3 else 1))
        for x in w:
            if x[0] in SB:
                st = x[3] if len(x) > 3 else 1
                hist[x[0]] = [y for y in hist[x[0]] if st > 1 or not (x[1] <= y[0] and y[1] <= x[2])] + [(x[1], x[2], i, True, st)]
        deps.discard(i)
        ops.append([q, KEY.get(q) if key is None else key, amount, fn, cost, sorted(deps | set(extra)), release, bias(r, w), sorted(deps)])
        return i

    def bias(r, w):
        h = 0 if any(x[0].endswith("_0") for x in list(r) + list(w)) else 1
        return PREF.get(cur[0] + str(h), 0.0) + (BIAS if h == 0 else 0.0)

    def width(x):
        return (x[2] - x[1] + (x[3] if len(x) > 3 else 1) - 1) // (x[3] if len(x) > 3 else 1)

    def half(*xs):
        return all(not psum(x) and PLACE[x[0]][2] in ("bfloat16", "float16", "uint16") for x in xs)

    def vcost(cyc):
        return CYC * max(64, cyc)

    def isap(s):
        return isinstance(s, tuple)

    def val(s):
        return ap(s) if isap(s) else s

    def tt(out, a, b, op):
        c = width(out) * (1 if psum(a) or psum(b) else 2)
        return add("V", vcost(c), lambda: g.vector.tensor_tensor(ap(out), ap(a), ap(b), op), [a, b], [out])

    def ts(out, a, s1, op0, s2=None, op1=None):
        c = width(out) * (0.5 if half(out, a) else 1)
        rd = [a] + [s for s in (s1, s2) if isap(s)]
        if op1 is None:
            return add("V", vcost(c), lambda: g.vector.tensor_scalar(ap(out), ap(a), val(s1), None, op0), rd, [out])
        return add("V", vcost(c), lambda: g.vector.tensor_scalar(ap(out), ap(a), val(s1), val(s2), op0, op1), rd, [out])

    def cp(out, a):
        c = width(out) * (0.5 if half(out, a) else 1)
        return add("V", vcost(c), lambda: g.vector.tensor_copy(ap(out), ap(a)), [a], [out])

    def fill(out, v):
        return add("V", vcost(width(out) * 0.5), lambda: g.vector.memset(ap(out), v), [], [out])

    def act(out, a, func, bias=0.0, scale=1.0):
        rd = [a] + [x for x in (bias, scale) if isap(x)]
        return add("A", vcost(width(out)), lambda: g.scalar.activation(ap(out), ap(a), func, bias=val(bias), scale=val(scale)), rd, [out])

    def times(out, a, s):
        return act(out, a, AF.Identity, scale=s)

    def agather(out, win, off, share):
        for q, a, b in (("V", 64 - share, 64), ("A", 0, 64 - share)):
            if a == b:
                continue
            o, f = (out[0], out[1] + 16 * a, out[1] + 16 * b), (off[0], off[1] + a, off[1] + b)

            def fn(q=q, o=o, f=f):
                if q == "V":
                    return g.vector.tensor_copy(ap(o), ap(win).indirect(ap(f)))
                return g.scalar.activation(ap(o), ap(win).indirect(ap(f)), AF.Copy)
            add(q, 0.06 + GC * CYC * width(o), fn, [win, f], [o])

    def vgather(out, win, off, b, op):
        return add("V", 0.05 + 1.56 * CYC * width(out),
                   lambda: g.vector.tensor_tensor(ap(out), ap(win).indirect(ap(off)), ap(b), op), [win, off, b], [out])

    def scatter(win, off, a):
        return add("V", 0.05 + 3.8 * CYC * width(a), lambda: g.vector.tensor_copy(ap(win).indirect(ap(off)), ap(a)), [off, a], [win])

    def mms(out, pairs):
        for j in range(len(pairs)):
            l, r = pairs[j]

            def fn(l=l, r=r, s=j == 0, e=j == len(pairs) - 1):
                return g.tensor.matmul(ap(out), ap(l), ap(r), s, e)
            add("T", PEC * max(64, width(out)), fn, [l, r], [out])

    def dma(out, a, cost=2.0):
        s = "dm%d" % ndma[0]
        ndma[0] += 1
        return add("S", cost, lambda: g.sync.dma_start(ap(out), ap(a)), [a], [out], key=s, amount=16)

    def send(dst, out, a, sem):
        rid, pid = topo.addr(dst, core)
        mask = topo.mask(core, dst)
        local[0] += len(topo.engines(core, dst))

        def fn():
            g.remote_dma(out_ap=ap(out), in_ap=ap(a), remote_sem=T.sem[sem], local_sem=T.sem.ls, pid=pid, routing_id=rid,
                         dma_engine_mask=mask)
        return add("G", 1.0, fn, [a], [], key="")

    def arrive(buf, sem, total, after=None, wait=0.0, release=0.0):
        add("X", wait, None, [], [buf], key=sem, amount=total, release=release, extra=() if after is None else (after,))

    def tolist(out, a, tmp, tmp2, plus=None):
        n2 = width(a)
        x, y = W(tmp, 0, n2), W(tmp2, 0, n2)
        tt(x, a, W("dg", 0, n2), OP.mult)
        add("V", vcost(n2 * (0.5 if half(x) else 1)),
            lambda: g.vector.tensor_tensor_scan(ap(y), ap(W("rs", 0, n2)), ap(x), 0.0, OP.mult, OP.add), [x, W("rs", 0, n2)], [y])
        if plus:
            ts(out, (tmp2, 15, n2, 16), plus, OP.add)
        else:
            cp(out, (tmp2, 15, n2, 16))

    def R(m, r):
        return (m, 15 - r, 143 - r)

    prev1 = T.cores[(rank - 1) % n]
    next1 = T.cores[(rank + 1) % n]

    dma(W("sli"), ("sl", 0, 128))
    dma(W("x"), ("x0", 0, 1024), 3.0)
    dma(W("zi"), ("z0", 0, 128))
    dma(W("wti"), ("wt", 0, 1))
    dma(W("kpi"), ("kp", 0, 1))
    dma(W("ce", 0, CUT), ("cl", 0, CUT), 4.0)
    dma(W("ce", CUT, NB), ("cl", CUT, NB), 4.0)
    dma(W("ce", NB, EXT), ("cl", 0, EXT - NB), 2.0)

    add("G", 0.14, lambda: g.iota(ap(W("pi")), [[0, 1]], 0, 1), [], [W("pi")])
    add("G", 0.4, lambda: g.iota(ap(W("ji")), [[1, 144]], 0, 0), [], [W("ji")])
    J128 = W("ji", 0, 128)
    cp(W("pf"), W("pi"))
    ts(W("pg"), W("pi"), 4, OP.arith_shift_right)
    ts(W("pq"), W("pi"), 15, OP.bitwise_and)
    cp(W("pgf"), W("pg"))
    cp(W("pqf"), W("pq"))
    ts(W("jg"), J128, 4, OP.arith_shift_right)
    ts(W("pwf"), W("pg"), 16.0, OP.mult, 15.0, OP.add)
    ts(W("id"), J128, W("pf"), OP.is_equal)
    ts(W("ih"), W("id"), 1.0, OP.mult)
    times(W("idn"), W("id"), -1.0)
    ts(W("bo"), W("jg"), W("pgf"), OP.is_equal)
    ts(W("wd"), W("ji"), W("pwf"), OP.is_equal)
    ts(W("oh"), W("ji", 0, 16), W("pqf"), OP.is_equal)
    times(W("ine"), W("id"), BIG)
    ts(W("gt"), J128, W("pf"), OP.is_gt)
    tt(W("lt"), W("gt"), W("bo"), OP.mult)
    ts(W("ta"), W("id"), -100.0, OP.mult)
    tt(W("ts"), W("ta"), W("lt"), OP.add)
    ts(W("jg"), J128, 15, OP.bitwise_and)
    ts(W("dg"), W("jg"), W("pqf"), OP.is_equal)
    ts(W("rs"), W("jg"), 0.5, OP.is_gt)
    ts(W("boh"), W("bo"), 1.0, OP.mult)
    fill(W("par"), 0.0)
    cp(W("par", 0, 1), W("wti"))
    cp(W("par", 1, 2), W("kpi"))
    fill(W("one"), 1.0)
    ts(W("cc"), W("oh", 0, 1), -0.5, OP.mult)
    ts(W("ccb"), W("oh", 1, 2), 2.0 ** -13, OP.mult)
    tt(W("cc"), W("cc"), W("ccb"), OP.add)
    ts(W("ca"), W("one"), W("cc"), OP.mult)

    def weights(t, src, c):
        ts(W("wq%d" % t), W("bo"), (src, c, c + 1), OP.mult, 2.0 ** -12, OP.mult)
        ts(W("kc%d" % t), (src, c + 1, c + 2), 2.0 ** 17, OP.mult)
    weights(0, "par", 0)
    times(W("id2"), W("id"), 2.0)
    times(W("id8"), W("id"), 8.0)
    times(W("id50"), W("id"), 50.0)
    times(W("bo50"), W("bo"), -50.0)
    times(W("bo05"), W("bo"), -0.5)
    times(W("bo100"), W("bo"), 100.0)
    times(W("tb"), W("id"), -8.0)
    times(W("tc"), W("lt"), 8.0)
    tt(W("te"), W("tb"), W("tc"), OP.add)
    times(W("wdf"), W("wd"), 0.5)
    ts(W("ihn"), W("id"), -1.0, OP.mult)
    ts(W("in8"), W("id"), -8.0, OP.mult)
    ts(W("tbc"), W("oh"), -1.0, OP.mult)
    ts(W("cb"), W("one", 0, 64), W("oh", 0, 1), OP.mult, -0.25, OP.mult)
    ts(W("cq"), W("one", 0, 64), W("oh", 0, 1), OP.mult, -7.0 / 16, OP.mult)
    fill(W("on32"), 1.0 / 32)
    fill(W("on16"), -1.0 / 16)
    cp(W("jb"), J128)
    ts(W("thr"), W("pqf"), KA - 0.5, OP.is_ge, -8.0, OP.mult)
    ts(W("thr"), W("thr"), 11.5, OP.add)
    ts(W("w7"), W("wti"), 7, OP.bitwise_and)
    ts(W("wa"), W("w7"), 3.5, OP.is_ge, -8.0, OP.mult)
    tt(W("w8"), W("wa"), W("w7"), OP.add)
    ts(W("b8"), W("bo"), W("w8"), OP.mult, 0.125, OP.mult)
    ts(W("b8x"), W("bo"), W("w8"), OP.mult)
    ts(W("bow"), W("bo"), W("par", 0, 1), OP.mult)
    ts(W("ohs"), W("oh"), -512.0, OP.mult)
    for k in range(16):
        times(W("bm", 128 * k, 128 * k + 128), W("bo"), W("ohs", k, k + 1))
    cp(W("kpb"), W("kpi"))
    mms(("ps_0", 72, 73), [(W("bm", 0, 128), W("kpb"))])
    ts(W("k0"), ("ps_0", 72, 73), -32.0 / 512, OP.mult)
    cur[0] = "t"
    add("G", 0.6, lambda: g.iota(ap(W("ul")), [[16, 256]], 0, 0), [], [W("ul")])
    add("G", 2.0, lambda: g.iota(ap(W("j1k")), [[0, 64], [1, 16]], 0, 0, allow_small_or_imprecise_dtypes=True), [], [W("j1k")])
    ts(W("rs1k"), W("j1k"), 0.5, OP.is_gt)
    ts(W("um2"), W("ul"), W("pqf"), OP.add)
    ts(W("uw2"), W("um2"), W("k0"), OP.add)
    tt(W("uy2"), W("uw2"), W("um2"), OP.mult)
    ts(W("uh"), W("uy2"), 5, OP.arith_shift_right, 4095, OP.bitwise_and)
    for t in range(VIS):
        ts(W("uo%d" % t), W("uh"), 97.0 * t, OP.add)
    cur[0] = "-"

    def own_book(t, after):
        if not CT[t]:
            return
        k = cur[0]
        cur[0] = "t"
        for c in range(8):
            out, win, off = W("ct%d" % t, 512 * c, 512 * c + 512), W("ce"), W("uo%d" % t, 32 * c, 32 * c + 32)
            add("A", 0.065 + GC * CYC * 512, lambda out=out, win=win, off=off:
                g.scalar.activation(ap(out), ap(win).indirect(ap(off)), AF.Copy), [win, off], [out], extra=[after])
        cur[0] = k

    def params(after):
        add("G", 2.0, fused, [W("par")], [], key="", extra=[after])
        local[0] += nsm

    def fused():
        dsts = [T.cores[(rank - 1 - t) % n] for t in range(1, VIS)]
        ids = []
        for d in dsts:
            rid, pid = topo.addr(d, core)
            ids.append(DstId(rid=rid, pnc=pid))
        outs = [ap(W("pr", 8 * t - 8, 8 * t)) for t in range(1, VIS)]
        g.remote_dma_fused([RemoteDMATransfer(dst_ids=ids, dma_engine_mask=topo.mask(core, dsts[0]), remote_sem=T.sem.pr,
                                              srcs=[ap(W("par"))], dsts=outs)], local_sem=T.sem.ls)
    nsm = len(topo.engines(core, prev1))
    arrive(W("pr"), "pr", nsm * (VIS - 1), release=12.0)

    def book(i, a, b, after):
        c = helpers(T, topo, rank)[i][0]
        rid, pid = topo.addr(c, core)
        e = onchip(T, topo, rank, c)

        def fn():
            g.remote_dma(out_ap=ap(W("hb", a, b)), in_ap=ap(W("ce", a, b)), remote_sem=T.sem.hb0, local_sem=T.sem.ls,
                         pid=pid, routing_id=rid, dma_engine_mask=sum(1 << x for x in e))
        add("G", 1.0, fn, [W("ce", a, b)], [], key="", extra=[after])
        local[0] += len(e)
    for t in range(1, VIS):
        arrive(W("bk%d" % t), "bk%d" % t, 2 * nsm, release=(0, 24.0, 32.0, 40.0, 48.0)[t])

    HV = range(2)
    for h in HV:
        s = "_%d" % h
        a, b = 64 * h, 64 * h + 64
        cp(W("sf" + s), W("sli", a, b))
        mms(("ps" + s, 80, 144), [(W("ih"), W("sf" + s))])
        act(W("zz" + s, 0, 64), W("zi", a, b), AF.Copy)
        act(W("zz" + s, 64, 128), W("zi", a, b), AF.Copy)
        mms(("pz" + s, 0, 64), [(W("id"), W("zz" + s, 0, 64))])

    def slots_in(s, first):
        SP = ("ps" + s, 80, 144)
        cp(W("so" + s), SP)
        act(W("em" + s), SP, AF.Relu, scale=-1.0)
        if not first:
            cp(W("sf" + s), SP)

    for h in HV:
        slots_in("_%d" % h, True)
    for t in range(VIS):
        CD, GE = ("cd", "ge") if t else ("ci", "gi")
        cur[0] = "g"
        for h in HV:
            s = "_%d" % h
            agather(W("o%d" % (t % 2) + s), W("x"), W("so" + s), VO[h])
        cur[0] = "d"
        for h in HV:
            s = "_%d" % h
            mms(("ps" + s, 0, 64), [(W("te"), W("em" + s)), (R("wdf", t), W("em" + s))])
            ts(W("d" + s), ("ps" + s, 0, 64), W("tbc", t, t + 1), OP.add, -0.9, OP.is_le)
        cur[0] = "o"
        for h in HV:
            s = "_%d" % h
            o, gg = "o%d" % (t % 2) + s, "gg" + s
            for k in range(KA, 16):
                c = 64 * (k - KA)
                mms(("pd" + s, c, c + 64), [(W("id"), (o, k, 1024, 16)), (W("idn"), W("zz" + s, 0, 64))])
            if KA < 16:
                act(W(gg, 64 * KA, 1024), ("pd" + s, 0, 64 * (16 - KA)), AF.Relu)
            for k in range(KA):
                tt(W(gg, 64 * k, 64 * k + 64), (o, k, 1024, 16), ("pz" + s, 0, 64), OP.is_gt)
            mms(("pn" + s, 0, 64), [(W("ine"), W("em" + s))] + [(R("wd", k), W(gg, 64 * k, 64 * k + 64)) for k in range(16)])
            ts(W("op" + s), ("pn" + s, 0, 64), 0.5, OP.is_gt)
        cur[0] = "s"
        for h in HV:
            s = "_%d" % h
            mms(("ps" + s, 0, 64), [(W("ts"), W("op" + s))])
            for j in range(2):
                c = 64 * j
                ts(W("se" + s, c, c + 64), ("ps" + s, 0, 64), -100.0 + j, OP.is_equal)
                tt(W("ss" + s, c, c + 64), W("se" + s, c, c + 64), ("ps" + s, 80, 144), OP.mult)
            mms(("ps" + s, 144, 272), [(W("boh"), W("ss" + s))])
            tolist(W("lo" + s), ("ps" + s, 144, 272), "lm" + s, "ls" + s)
            vgather(W(CD + s), W("x"), W("lo" + s), W("zz" + s), OP.min)
            if t == 0:
                i = send(next1, W("rc" + s), W(CD + s), "rc%d" % h)
                arrive(W("rc" + s), "rc%d" % h, nsm, after=i, wait=MSG)
        if t == 0:
            book(0, 0, CUT, i)
            book(1, CUT, EXT, i)
            params(i)
            own_book(0, i)
        cur[0] = "h"
        for h in HV:
            s = "_%d" % h
            cs = W(("cd" if t else "rc") + s)
            wq = W("wq%d" % t)
            if t and h == 0:
                weights(t, "pr", 8 * t - 8)
            mms(("ps" + s, 144, 272), [(W("bo"), W("ca")), (wq, cs)])
            ts(W("qb" + s), ("ps" + s, 144, 272), MG, OP.add, MG, OP.subtract)
            mms(("ps" + s, 272, 400), [(wq, cs), (W("idn"), W("qb" + s))])
            mms(("pz" + s, 64, 192), [(W("id"), cs)])
            act(W("ww" + s), ("ps" + s, 272, 400), AF.Identity, bias=W("kc%d" % t), scale=2.0 ** 24)
            tt(W("y" + s), W("ww" + s), ("ps" + s, 272, 400), OP.mult)
            ts(W("y2" + s), W("y" + s), 5, OP.arith_shift_right, 4095, OP.bitwise_and)
            cp(W("ho" + s), W("y2" + s))
        cur[0] = "b"
        for h in HV:
            s = "_%d" % h
            win = W("bk%d" % t) if t else W("ce", 0, NB)
            for j in range(2):
                c = 64 * j
                agather(W("b" + s, 1024 * j, 1024 * j + 1024), win, W("ho" + s, c, c + 64), VB[2 * h + j])
                last = len(ops) - 1
                for m in range(16):
                    e = 1024 * j + 64 * m
                    tt(W("gb" + s, e, e + 64), ("b" + s, 1024 * j + m, 1024 * j + 1024, 16), ("pz" + s, 64 + c, 128 + c), OP.is_le)
                mms(("pn" + s, 64 + c, 128 + c), [(R("wd", m), W("gb" + s, 1024 * j + 64 * m, 1024 * j + 64 * m + 64)) for m in range(16)])
                ts(W(GE + s, c, c + 64), ("pn" + s, 64 + c, 128 + c), 8.5, OP.is_ge)
            if t < VIS - 1 and h == 1:
                own_book(t + 1, last)
            if t == 0:
                i = send(prev1, W("rg" + s), W(GE + s), "rg%d" % h)
                arrive(W("rg" + s), "rg%d" % h, nsm, after=i, wait=MSG)
        cur[0] = "v"
        for h in HV:
            s = "_%d" % h
            PS = "ps" + s
            ge, se, ng = ("ge" if t else "rg") + s, "se" + s, "ng" + s
            thr = 99.5 + AT[t]
            zz = W("zz" + s, 0, 64)
            mms((PS, 144, 272), [(W("id"), W(CD + s)), (W("idn"), W("zz" + s))])
            mms((PS, 272, 336), [(W("id"), W(se, 0, 64)), (W("idn"), W("d" + s))])
            mms((PS, 336, 400), [(W("id"), W(se, 64, 128)), (W("idn"), W("d" + s))])
            bits = [(W("id"), W("rb%d" % t + s))] if t else []
            mms((PS, 0, 64), [(W("bo100"), W(se, 0, 64)), (W("bo"), W(ge, 0, 64))] + bits)
            ts(W(ng, 0, 64), (PS, 0, 64), thr, OP.is_ge)
            mms((PS, 400, 464), [(W("bo"), W("cb")), (W("on32"), W(ng, 0, 64))])
            mms((PS, 0, 64), [(W("bo50"), W(se, 64, 128)), (W("bo05"), W(ge, 64, 128)), (W("id50"), W(ng, 0, 64)), (W("on32"), W(ng, 0, 64))])
            ts(W("qn" + s), (PS, 400, 464), MG, OP.add, MG + (100 + AT[t]) // 2, OP.subtract)
            tt(W(ng, 64, 128), W("qn" + s), (PS, 0, 64), OP.is_gt if AT[t] % 2 else OP.is_ge)
            for j in range(2):
                c = 64 * j
                tt(W("pp" + s, c, c + 64), W(ng, c, c + 64), (PS, 144 + c, 208 + c), OP.mult)
                tt(W("mp" + s, c, c + 64), W(ng, c, c + 64), (PS, 272 + c, 336 + c), OP.mult)
            mms(("pz" + s, 192, 256), [(W("id"), zz), (W("id"), W("pp" + s, 0, 64)), (W("id"), W("pp" + s, 64, 128))])
            cp(W("m" + s), ("pz" + s, 192, 256))
        cur[0] = "n"
        for h in HV:
            s = "_%d" % h
            PS = "ps" + s
            parts = [W("zz" + s, 0, 64), W("pp" + s, 0, 64), W("pp" + s, 64, 128)]
            mms((PS, 208, 272), [(W("bo"), W("cq"))] + [(W("b8"), x) for x in parts])
            ts(W("qf" + s), (PS, 208, 272), MG, OP.add, MG, OP.subtract)
            mms((PS, 144, 208), [(W("id"), W("d" + s)), (W("id"), W("mp" + s, 0, 64)), (W("id"), W("mp" + s, 64, 128))])
            cp(W("pm" + s), (PS, 144, 208))
            nn = [(W("b8x"), W("m" + s)), (W("id8"), W("jb", 64 * h, 64 * h + 64)), (W("in8"), W("qf" + s))]
            mms((PS, 272, 336), nn)
            mms((PS, 336, 400), nn + [(W("ihn"), W("sf" + s))])
            tolist(W("no" + s, 0, 4), (PS, 272, 336), "lm" + s, "ls" + s)
            scatter(W("x"), W("no" + s, 0, 4), W("m" + s))
            tt(W("tt" + s), W("pm" + s), (PS, 336, 400), OP.mult)
            mms((PS, 80, 144), [(W("ih"), W("sf" + s)), (W("ih"), W("tt" + s))])
        cur[0] = "j"
        if t < VIS - 1:
            for h in HV:
                s = "_%d" % h
                PS, ng = "ps" + s, "ng" + s
                mms((PS, 400, 464), [(W("bo"), W("cb")), (W("on32"), W(ng, 64, 128))])
                ts(W("qn2" + s), (PS, 400, 464), MG, OP.add, MG, OP.subtract)
                mms((PS, 0, 64), [(W("on16"), W(ng, 64, 128)), (W("id2"), W("qn2" + s))])
                act(W("bs%d" % (t + 1) + s), (PS, 0, 64), AF.Copy)
                i = send(prev1, W("rb%d" % (t + 1) + s), W("bs%d" % (t + 1) + s), "rb%d" % (t + 1) + s)
                arrive(W("rb%d" % (t + 1) + s), "rb%d" % (t + 1) + s, nsm, after=i, wait=MSG)
        cur[0] = "r"
        for h in HV:
            s = "_%d" % h
            o, gg = "o%d" % (t % 2) + s, "gg" + s
            for k in range(KA, 16):
                c = 64 * (k - KA)
                mms(("pd" + s, c, c + 64), [(W("idn"), (o, k, 1024, 16)), (W("id"), W("m" + s))])
            if KA < 16:
                act(W(gg, 64 * KA, 1024), ("pd" + s, 0, 64 * (16 - KA)), AF.Sign, bias=0.5)
            for k in range(KA):
                tt(W(gg, 64 * k, 64 * k + 64), (o, k, 1024, 16), ("pz" + s, 192, 256), OP.is_le)
            mms(("pn" + s, 0, 64), [(W("ine"), W("em" + s))]
                + [(R("wd" if k < KA else "wdf", k), W(gg, 64 * k, 64 * k + 64)) for k in range(16)])
            ts(W("nn" + s), ("pn" + s, 0, 64), W("thr"), OP.is_lt)
        cur[0] = "i"
        for h in HV:
            s = "_%d" % h
            if t < VIS - 1:
                slots_in(s, False)
            else:
                cp(W("yl" + s), ("ps" + s, 80, 144))
                dma(("yl", 64 * h, 64 * h + 64), W("yl" + s))
        if t == VIS - 1:
            dma(("yx", 0, 1024), W("x"))
        cur[0] = "c"
        for h in HV:
            s = "_%d" % h
            o = "o%d" % (t % 2) + s
            for k in range(16):
                p = ("pd" if k < 8 else "pn") + s
                c = 64 * (k % 8)
                mms((p, c, c + 64), [(W("id"), (o, k, 1024, 16)), (W("bm", 128 * k, 128 * k + 128), W("nn" + s))])
            for k in range(16):
                p = (("pd" if k < 8 else "pn") + s, 64 * (k % 8), 64 * (k % 8) + 64)
                if k < KR:
                    act(("mo" + s, k, 1024, 16), p, AF.Relu)
                else:
                    ts(("mo" + s, k, 1024, 16), p, 0.0, OP.max)
            add("V", vcost(512), lambda s=s: g.vector.tensor_tensor_scan(ap(W("ms" + s)), ap(W("rs1k")), ap(W("mo" + s)), 0.0,
                                                                        OP.mult, OP.max), [W("rs1k"), W("mo" + s)], [W("ms" + s)])
            tt(W("c" + s), ("ms" + s, 15, 1024, 16), ("pz" + s, 192, 256), OP.max)
        cur[0] = "z"
        for h in HV:
            s = "_%d" % h
            PS = "ps" + s
            mms((PS, 0, 64), [(W("bow"), W("c" + s))])
            cp(W("ui" + s), (PS, 0, 64))
            ts(W("uj" + s), W("ui" + s), 4095, OP.bitwise_and)
            if CT[t]:
                tolist(W("co" + s, 0, 4), W("uj" + s), "um" + s, "us" + s)
                vgather(W("df" + s), W("ct%d" % t), W("co" + s, 0, 4), W("c" + s), OP.subtract)
            else:
                ts(W("uw" + s), W("uj" + s), W("k0"), OP.add)
                tt(W("uy" + s), W("uw" + s), W("uj" + s), OP.mult)
                ts(W("uz" + s), W("uy" + s), 5, OP.arith_shift_right, 4095, OP.bitwise_and)
                tolist(W("co" + s, 0, 4), W("uz" + s), "um" + s, "us" + s, 97.0 * t)
                vgather(W("df" + s), W("ce"), W("co" + s, 0, 4), W("c" + s), OP.subtract)
            if t < VIS - 1:
                act(("pz" + s, 0, 64), W("df" + s), AF.Abs)
            act(W("zz" + s, 0, 64), W("df" + s), AF.Abs)
            if t < VIS - 1:
                act(W("zz" + s, 64, 128), W("df" + s), AF.Abs)
            else:
                dma(("yz", 64 * h, 64 * h + 64), W("zz" + s, 0, 64))

    if "order" not in ORDER:
        ORDER["order"] = schedule(ops)
    known = {q: {} for q in QUEUE}
    count, clock = {}, {}
    for i in ORDER["order"]:
        q, key, amount, fn, _c, _e, _r, _b, deps = ops[i]
        if q == "X":
            clock[i] = {key: amount}
            count[key] = amount
            continue
        k = known[q]
        need = {}
        for d in deps:
            if ops[d][0] == "T" and q == "T":
                continue
            kd = ops[d][1]
            if kd == "" or kd is None:
                continue
            v = clock[d][kd]
            if k.get(kd, 0) < v and need.get(kd, (0, 0))[0] < v:
                need[kd] = (v, d)
        for kd in list(need):
            v, d = need[kd]
            for k2 in need:
                if k2 != kd and clock[need[k2][1]].get(kd, 0) >= v:
                    del need[kd]
                    break
        for kd in need:
            v, d = need[kd]
            QUEUE[q].wait_ge(T.sem[kd], v)
            for kk in clock[d]:
                if k.get(kk, 0) < clock[d][kk]:
                    k[kk] = clock[d][kk]
        ins = fn()
        c = dict(k)
        if key:
            count[key] = count.get(key, 0) + amount
            ins.then_inc(T.sem[key], amount)
            c[key] = count[key]
        clock[i] = c
    for key in sorted(count):
        g.wait_ge(T.sem[key], count[key])
    g.wait_ge(T.sem.ls, local[0])


def schedule(ops):
    m = len(ops)
    users = [[] for _ in range(m)]
    left = [0] * m
    for i in range(m):
        for d in ops[i][5]:
            users[d].append(i)
            left[i] += 1
    tail = [0.0] * m
    for i in range(m - 1, -1, -1):
        tail[i] = ops[i][4] + max([HOP + tail[u] for u in users[i]] + [0.0])
    free = {"V": 0.0, "A": 0.0, "T": 0.0, "G": 0.0, "S": 0.0}
    ready = {q: [] for q in free}
    est = [ops[i][6] for i in range(m)]
    order, start = [], [0.0] * m
    work = [i for i in range(m) if left[i] == 0]

    def done(i, end):
        for u in users[i]:
            est[u] = max(est[u], end + (0.0 if ops[i][0] == "T" and ops[u][0] == "T" else HOP))
            left[u] -= 1
            if left[u] == 0:
                work.append(u)

    while True:
        while work:
            i = work.pop()
            if ops[i][0] == "X":
                start[i] = est[i]
                order.append(i)
                done(i, est[i] + ops[i][4])
            else:
                ready[ops[i][0]].append(i)
        best = None
        for q in ready:
            if ready[q]:
                t0 = max(free[q], min(est[i] for i in ready[q]))
                if best is None or t0 < best[0]:
                    best = (t0, q)
        if best is None:
            break
        t0, q = best
        i = max((j for j in ready[q] if est[j] <= t0), key=lambda j: (tail[j] + ops[j][7], -j))
        ready[q].remove(i)
        start[i] = t0
        order.append(i)
        end = t0 + ops[i][4]
        free[q] = t0 + (0.1 if q == "S" else ops[i][4])
        done(i, end)
    ORDER["span"] = max(start[i] + ops[i][4] for i in range(m))
    ORDER["start"] = start
    return order
